import numpy as np
import ml_dtypes


def mxq(x, axis, fmt="e4m3"):
    dtype, down = {"e4m3": (ml_dtypes.float8_e4m3fn, 7), "e5m2": (ml_dtypes.float8_e5m2, 14)}[fmt]
    v = np.moveaxis(np.asarray(x, np.float32).astype(ml_dtypes.bfloat16).astype(np.float64), axis, -1)
    blocks = v.reshape(v.shape[:-1] + (-1, 32))
    amax = np.abs(blocks).max(-1, keepdims=True)
    byte = np.maximum(np.where(amax > 0, np.frexp(amax)[1] - 1 + 127, 0) - down, 1)
    scale = np.exp2(byte - 127.0)
    codes = (blocks / scale).astype(np.float32).astype(dtype).astype(np.float64)
    return np.moveaxis((codes * scale).reshape(v.shape), -1, axis)


WIDE = False


def mx_kscale(k):
    if not WIDE:
        return np.ones(k)
    levels = np.array([10, -10, 5, -5, 0])
    if k % 512:
        return np.exp2(np.random.permutation(np.resize(levels, k // 32))).repeat(32)
    a = np.empty((k // 512, 16))
    for p in range(k // 512):
        a[p, :8] = np.random.permutation(np.resize(levels, 8))
        for g in range(8):
            far = levels[np.abs(levels - a[p, g]) >= 10]
            a[p, g + 8] = far[np.random.randint(len(far))]
    return np.exp2(a.ravel()).repeat(32)


def f64(x):
    return np.asarray(x).astype(np.float64)


def striped(idx):
    return np.tile(idx.reshape(-1, 16).T, (8, 1)).astype(np.uint16)


def unstriped(offs):
    return offs[:16].T.reshape(-1).astype(np.int64)


E2M1 = np.array([0.0, 0.5, 1.0, 1.5, 2.0, 3.0, 4.0, 6.0, -0.0, -0.5, -1.0, -1.5, -2.0, -3.0, -4.0, -6.0])


def pack_weight(w, fmt):
    k, n = w.shape
    w = f64(np.asarray(w, np.float32).astype(ml_dtypes.bfloat16)).reshape(k // 32, 32, n)
    amax = np.abs(w).max(1)
    if fmt == "e4m3":
        byte = np.frexp(amax)[1] - 1 + 127 - 7
    else:
        mant, ex = np.frexp(amax / 6.0)
        byte = np.where(mant > 0.5, ex, ex - 1) + 127
    byte = np.clip(np.where(amax > 0, byte, 1), 1, 254)
    scaled = (w * np.exp2(127.0 - byte)[:, None, :]).reshape(k, n).astype(np.float32)
    by_word = np.ascontiguousarray(scaled.reshape(k // 512, 128, 4, n).transpose(0, 1, 3, 2))
    if fmt == "e4m3":
        words = by_word.astype(ml_dtypes.float8_e4m3fn).view(np.uint8)
    else:
        c = by_word.astype(ml_dtypes.float4_e2m1fn).view(np.uint8) & 0xF
        words = (c[..., 0::2] | (c[..., 1::2] << 4)).reshape(k // 512, 128, 2 * n)
    return np.ascontiguousarray(words), np.ascontiguousarray(byte.astype(np.uint8).reshape(k // 512, 16, n))


def unpack_weight(words, scales, fmt):
    g, _, n = scales.shape
    words = np.ascontiguousarray(words).reshape(g, 128, n, -1)
    if fmt == "e4m3":
        vals = words.view(ml_dtypes.float8_e4m3fn).astype(np.float64)
    else:
        nib = np.empty((g, 128, n, 4), np.uint8)
        nib[..., 0::2] = words & 0xF
        nib[..., 1::2] = words >> 4
        vals = E2M1[nib]
    vals = vals * np.repeat(np.exp2(scales.astype(np.float64) - 127.0), 8, axis=1)[..., None]
    return vals.transpose(0, 1, 3, 2).reshape(g * 512, n)


def relu(v):
    return np.maximum(v, 0.0)


K, T, E, N = 512, 1536, 12, 128
COUNTS = (128, 128, 128, 128, 384, 128, 256, 512, 128, 256, 512, 384)
STARTS = np.cumsum((0,) + COUNTS)


def by_expert(wq, xq):
    return np.concatenate([wq[e].T @ xq[:, STARTS[e]:STARTS[e + 1]] for e in range(E)], axis=1)


def setup_inputs():
    n = np.random.standard_normal
    s = mx_kscale(K)[:, None]
    both = np.repeat(np.arange(E), COUNTS)
    pair = np.stack([both[:T], both[T:]])[:, np.random.permutation(T)]
    pair = np.where(np.random.rand(T) < 0.5, pair, pair[::-1])
    for _ in range(8):
        s_, t_ = np.random.permutation(T).reshape(2, -1); r = np.random.randint(2, size=T // 2); q = np.random.randint(2, size=T // 2); x, y = pair[r, s_].copy(), pair[q, t_].copy()
        ok = (pair[1 - r, s_] != y) & (pair[1 - q, t_] != x); pair[r[ok], s_[ok]] = y[ok]; pair[q[ok], t_[ok]] = x[ok]
    order = np.argsort(pair.reshape(-1), kind="stable")
    slot_token = order % T; pos = np.empty(2 * T, np.int64); pos[order] = np.arange(2 * T); pos = pos.reshape(2, T)
    g = np.random.uniform(0.2, 0.8, T)
    w = [pack_weight(m, "e2m1") for m in n((E, K, N)) / np.sqrt(K) / s[None]]
    return {
        "xT": (n((K, T)) * s).astype(np.float32),
        "w_words": np.stack([m[0] for m in w]),
        "w_scales": np.stack([m[1] for m in w]),
        "b": (0.3 * n((N, E))).astype(np.float32),
        "gate": np.stack([np.tile(g, (N, 1)), np.tile(1.0 - g, (N, 1))]).astype(np.float32),
        "offs": striped(slot_token),
        "pos1": striped(pos[0]),
        "pos2": striped(pos[1]),
    }


def reference(xT, w_words, w_scales, b, gate, offs, pos1, pos2):
    idx = unstriped(offs)
    w = np.stack([unpack_weight(w_words[e], w_scales[e], "e2m1") for e in range(E)])
    xq = mxq(f64(xT)[:, idx], 0, "e4m3")
    y = by_expert(w, xq)
    y = relu(y + np.repeat(f64(b), COUNTS, axis=1))
    return f64(gate[0]) * y[:, unstriped(pos1)] + f64(gate[1]) * y[:, unstriped(pos2)]

@@ -1,0 +1,152 @@
+from contextlib import ExitStack
+
+import concourse.mybir as mybir
+
+K, T, E, N = 512, 1536, 12, 128
+COUNTS = (128, 128, 128, 128, 384, 128, 256, 512, 128, 256, 512, 384)
+S = 3072
+
+P = 128
+PACK = 4
+F32 = mybir.dt.float32
+BF16 = mybir.dt.bfloat16
+U32 = mybir.dt.uint32
+I32 = mybir.dt.int32
+U16 = mybir.dt.uint16
+U8 = mybir.dt.uint8
+E4M3X4 = mybir.dt.float8_e4m3fn_x4
+E2M1X4 = mybir.dt.float4_e2m1fn_x4
+RELU = mybir.ActivationFunctionType.Relu
+ADD = mybir.AluOpType.add
+MAX = mybir.AluOpType.max
+MULT = mybir.AluOpType.mult
+
+FLOPS = 2 * S * K * N
+
+LOADS = ((0, 1024), (1024, 256), (1280, 256))
+CHUNKS = ((0, 512, 304), (512, 512, 304), (1024, 256, 144), (1280, 256, 160))
+CODE_GATHERS = ((0, 1024), (1024, 1152), (2176, 640), (2816, 256))
+SCALE_GATHERS = CODE_GATHERS
+PIECES = (
+    ((0, 0, 128, 0, 0), (1, 128, 128, 0, 128), (2, 256, 128, 0, 256), (3, 384, 128, 0, 384),
+     (4, 512, 384, 1, 0), (5, 896, 128, 1, 384)),
+    ((6, 1024, 256, 2, 0), (8, 1792, 128, 2, 256), (7, 1280, 512, 3, 0), (9, 1920, 256, 4, 0)),
+    ((10, 2176, 512, 5, 0), (11, 2688, 128, 6, 0)),
+    ((11, 2816, 128, 7, 0), (11, 2944, 128, 0, 0)),
+)
+OUT_SPLIT = ((0, 960), (960, 352), (1312, 224))
+
+
+def widths(slots):
+    return {128: (128,), 256: (256,), 384: (256, 128), 512: (512,)}[slots]
+
+
+def tile_moe_rag_lin_relu_kernel(tc, xT, w_words, w_scales, b, gate, offs, pos1, pos2, out):
+    nc = tc.nc
+    with ExitStack() as ctx:
+        lists = ctx.enter_context(tc.tile_pool(name="lists", bufs=1))
+        keep = ctx.enter_context(tc.tile_pool(name="keep", bufs=1))
+        psum = ctx.enter_context(tc.psum_pool(name="psum", bufs=1))
+
+        idx = lists.tile([P, 2 * T // 16], U16, name="idx")
+        p1 = lists.tile([P, T // 16], U16, name="p1")
+        p2 = lists.tile([P, T // 16], U16, name="p2")
+
+        codes = keep.tile([P, T], U32, name="codes", align_bytes=64)
+        scales = keep.tile([P, T], U8, name="scales", align_bytes=64)
+        slot_codes = keep.tile([P, S], U32, name="slot_codes", align_bytes=64)
+        slot_scales = keep.tile([P, S], U8, name="slot_scales", align_bytes=64)
+        wt = keep.tile([P, E, 2 * N], U8, name="wt", align_bytes=64)
+        wt_scales = keep.tile([P, E, N], U8, name="wt_scales", align_bytes=64)
+        bias = keep.tile([P, E], F32, name="bias")
+        gates = keep.tile([P, 2, T], F32, name="gates")
+        y = keep.tile([P, S], F32, name="y")
+        first = keep.tile([P, T], F32, name="first")
+        second = keep.tile([P, T], F32, name="second")
+        total = keep.tile([P, T], F32, name="total")
+        warm = keep.tile([P, 1], F32, name="warm")
+
+        nc.gpsimd.memset(warm[:], 0.0)
+        nc.scalar.activation(warm[:], warm[:], RELU)
+        nc.gpsimd.memset(scales[:], 0)
+        nc.vector.memset(wt_scales[:].rearrange("p e n -> p (e n)").bitcast(I32), 0)
+
+        rows = xT.rearrange("(p j) t -> p j t", j=PACK)
+        raw = []
+        for i, (t0, n) in enumerate(LOADS):
+            r = keep.tile([P, PACK, n], F32, name=f"raw{i}")
+            nc.sync.dma_start(out=r[:], in_=rows[:, :, t0 : t0 + n])
+            raw += [(r, c0 - t0) for c0, m, v in CHUNKS if t0 <= c0 < t0 + n]
+        nc.sync.dma_start(idx[:], offs)
+        w_scales_i = w_scales.bitcast(I32)
+        for q in range(4):
+            nc.sync.dma_start(
+                out=wt_scales[32 * q : 32 * q + 4].bitcast(I32),
+                in_=w_scales_i[:, 0, 4 * q : 4 * q + 4, :].rearrange("e q n -> q e n"),
+            )
+        nc.sync.dma_start(out=wt[:].bitcast(I32), in_=w_words.bitcast(I32).rearrange("e a p c -> p (e a) c"))
+        nc.sync.dma_start(out=bias[:], in_=b)
+        nc.sync.dma_start(p1[:], pos1)
+        nc.sync.dma_start(p2[:], pos2)
+        nc.sync.dma_start(out=gates[:], in_=gate.rearrange("c p t -> p c t"))
+
+        grouped = []
+
+        def quantize(i):
+            t0, n, v = CHUNKS[i]
+            nc.vector.quantize_mx(
+                out=codes[:, t0 : t0 + n].bitcast(E4M3X4),
+                scales=scales[:, t0 : t0 + n],
+                in_=grouped[i][:].rearrange("p t j -> p (t j)"),
+            )
+
+        for i, (t0, n, v) in enumerate(CHUNKS):
+            r, c = raw[i]
+            g = keep.tile([P, n, PACK], BF16, name=f"grouped{i}", align_bytes=64)
+            nc.vector.tensor_copy(
+                g[:, :v, :].rearrange("p (q i) j -> p q j i", i=4), r[:, :, c : c + v].rearrange("p j (q i) -> p q j i", i=4)
+            )
+            nc.scalar.copy(
+                g[:, v:, :].rearrange("p (q i) j -> p q j i", i=4), r[:, :, c + v : c + n].rearrange("p j (q i) -> p q j i", i=4)
+            )
+            grouped.append(g)
+            if i > 0:
+                quantize(i - 1)
+        quantize(len(CHUNKS) - 1)
+
+        banks = [psum.tile([P, 512], F32, name=f"bank{i}") for i in range(8)]
+        for gi, (s0, n) in enumerate(SCALE_GATHERS):
+            if gi < len(CODE_GATHERS):
+                c0, m = CODE_GATHERS[gi]
+                nc.vector.tensor_copy(slot_codes[:, c0 : c0 + m], codes[:].indirect(idx[:, c0 // 16 : (c0 + m) // 16]))
+            nc.vector.tensor_copy(slot_scales[:, s0 : s0 + n], scales[:].indirect(idx[:, s0 // 16 : (s0 + n) // 16]))
+            for e, a, m, bank, c in PIECES[gi]:
+                d = 0
+                for w in widths(m):
+                    nc.tensor.matmul_mx(
+                        out=banks[bank][:, c + d : c + d + w],
+                        lhsT=wt[:, e, :].bitcast(E2M1X4),
+                        lhsT_scale=wt_scales[:, e, :],
+                        rhs=slot_codes[:, a + d : a + d + w].bitcast(E4M3X4),
+                        rhs_scale=slot_scales[:, a + d : a + d + w],
+                        start=True,
+                        stop=True,
+                    )
+                    d += w
+            for e, a, m, bank, c in PIECES[gi]:
+                if a + m == S:
+                    nc.vector.tensor_scalar(y[:, a : a + m], banks[bank][:, c : c + m], bias[:, e : e + 1], 0.0, ADD, MAX)
+                else:
+                    nc.scalar.activation(y[:, a : a + m], banks[bank][:, c : c + m], RELU, bias=bias[:, e : e + 1])
+
+        nc.vector.tensor_tensor(first[:], y[:].indirect(p1[:]), gates[:, 0, :], MULT)
+        for i in range(len(OUT_SPLIT) + 1):
+            if i < len(OUT_SPLIT):
+                t0, n = OUT_SPLIT[i]
+                cols = slice(t0, t0 + n)
+                nc.vector.tensor_tensor(second[:, cols], y[:].indirect(p2[:, t0 // 16 : (t0 + n) // 16]), gates[:, 1, cols], MULT)
+            if i > 0:
+                t0, n = OUT_SPLIT[i - 1]
+                cols = slice(t0, t0 + n)
+                nc.vector.tensor_tensor(total[:, cols], first[:, cols], second[:, cols], ADD)
+                nc.sync.dma_start(out=out[:, cols], in_=total[:, cols])

@@ -1,6 +1,7 @@
 from contextlib import ExitStack
 
 import concourse.mybir as mybir
+from concourse.masks import make_identity
 
 K, T, E, N = 512, 1536, 12, 128
 COUNTS = (128, 128, 128, 128, 384, 128, 256, 512, 128, 256, 512, 384)
@@ -34,7 +35,8 @@ PIECES = (
     ((10, 2176, 512, 5, 0), (11, 2688, 128, 6, 0)),
     ((11, 2816, 128, 7, 0), (11, 2944, 128, 0, 0)),
 )
-OUT_SPLIT = ((0, 960), (960, 352), (1312, 224))
+PE_SUMS = ((0, 256), (256, 256), (512, 256), (768, 256))
+VECTOR_SUMS = ((1024, 224), (1248, 160), (1408, 128))
 
 
 def widths(slots):
@@ -69,6 +71,9 @@ def tile_moe_rag_lin_relu_kernel(tc, xT, w_words, w_scales, b, gate, offs, pos1,
         nc.gpsimd.memset(warm[:], 0.0)
         nc.scalar.activation(warm[:], warm[:], RELU)
         nc.gpsimd.memset(scales[:], 0)
+        ident = keep.tile([P, P], F32, name="ident")
+        make_identity(nc, ident[:])
+        turned = keep.tile([P, T], F32, name="turned")
         nc.vector.memset(wt_scales[:].rearrange("p e n -> p (e n)").bitcast(I32), 0)
 
         rows = xT.rearrange("(p j) t -> p j t", j=PACK)
@@ -139,14 +144,30 @@ def tile_moe_rag_lin_relu_kernel(tc, xT, w_words, w_scales, b, gate, offs, pos1,
                 else:
                     nc.scalar.activation(y[:, a : a + m], banks[bank][:, c : c + m], RELU, bias=bias[:, e : e + 1])
 
-        nc.vector.tensor_tensor(first[:], y[:].indirect(p1[:]), gates[:, 0, :], MULT)
-        for i in range(len(OUT_SPLIT) + 1):
-            if i < len(OUT_SPLIT):
-                t0, n = OUT_SPLIT[i]
-                cols = slice(t0, t0 + n)
-                nc.vector.tensor_tensor(second[:, cols], y[:].indirect(p2[:, t0 // 16 : (t0 + n) // 16]), gates[:, 1, cols], MULT)
+        def product(dst, pos, choice, t0, n):
+            cols = slice(t0, t0 + n)
+            nc.vector.tensor_tensor(dst[:, cols], y[:].indirect(pos[:, t0 // 16 : (t0 + n) // 16]), gates[:, choice, cols], MULT)
+
+        for i, (t0, n) in enumerate(PE_SUMS):
+            product(first, p1, 0, t0, n)
+            product(second, p2, 1, t0, n)
+            cols = slice(t0, t0 + n)
+            there, back = banks[2 * i], banks[2 * i + 1]
+            for d in range(0, n, P):
+                block = slice(t0 + d, t0 + d + P)
+                nc.tensor.matmul(there[:, d : d + P], first[:, block], ident[:], start=True, stop=False, is_transpose=True)
+                nc.tensor.matmul(there[:, d : d + P], second[:, block], ident[:], start=False, stop=True, is_transpose=True)
+            nc.scalar.copy(turned[:, cols], there[:, :n])
+            for d in range(0, n, P):
+                nc.tensor.transpose(back[:, d : d + P], turned[:, t0 + d : t0 + d + P], ident[:])
+            nc.scalar.copy(total[:, cols], back[:, :n])
+            nc.sync.dma_start(out=out[:, cols], in_=total[:, cols])
+        product(first, p1, 0, VECTOR_SUMS[0][0], T - VECTOR_SUMS[0][0])
+        for i in range(len(VECTOR_SUMS) + 1):
+            if i < len(VECTOR_SUMS):
+                product(second, p2, 1, *VECTOR_SUMS[i])
             if i > 0:
-                t0, n = OUT_SPLIT[i - 1]
+                t0, n = VECTOR_SUMS[i - 1]
                 cols = slice(t0, t0 + n)
                 nc.vector.tensor_tensor(total[:, cols], first[:, cols], second[:, cols], ADD)
                 nc.sync.dma_start(out=out[:, cols], in_=total[:, cols])

@@ -35,8 +35,8 @@ PIECES = (
     ((10, 2176, 512, 5, 0), (11, 2688, 128, 6, 0)),
     ((11, 2816, 128, 7, 0), (11, 2944, 128, 0, 0)),
 )
-PE_SUMS = ((0, 256), (256, 256), (512, 256), (768, 256))
-VECTOR_SUMS = ((1024, 224), (1248, 160), (1408, 128))
+PE_SUMS = ((0, 256), (256, 384))
+VECTOR_SUMS = ((640, 384), (1024, 288), (1312, 224))
 
 
 def widths(slots):
@@ -148,9 +148,9 @@ def tile_moe_rag_lin_relu_kernel(tc, xT, w_words, w_scales, b, gate, offs, pos1,
             cols = slice(t0, t0 + n)
             nc.vector.tensor_tensor(dst[:, cols], y[:].indirect(pos[:, t0 // 16 : (t0 + n) // 16]), gates[:, choice, cols], MULT)
 
+        product(first, p1, 0, 0, VECTOR_SUMS[0][0])
+        product(second, p2, 1, 0, VECTOR_SUMS[0][0])
         for i, (t0, n) in enumerate(PE_SUMS):
-            product(first, p1, 0, t0, n)
-            product(second, p2, 1, t0, n)
             cols = slice(t0, t0 + n)
             there, back = banks[2 * i], banks[2 * i + 1]
             for d in range(0, n, P):

@@ -35,8 +35,8 @@ PIECES = (
     ((10, 2176, 512, 5, 0), (11, 2688, 128, 6, 0)),
     ((11, 2816, 128, 7, 0), (11, 2944, 128, 0, 0)),
 )
-PE_SUMS = ((0, 256), (256, 384))
-VECTOR_SUMS = ((640, 384), (1024, 288), (1312, 224))
+PE_SUMS = ((0, 128), (128, 256))
+VECTOR_SUMS = ((384, 576), (960, 352), (1312, 224))
 
 
 def widths(slots):
@@ -139,7 +139,7 @@ def tile_moe_rag_lin_relu_kernel(tc, xT, w_words, w_scales, b, gate, offs, pos1,
                     )
                     d += w
             for e, a, m, bank, c in PIECES[gi]:
-                if a + m == S:
+                if a + m == S - P:
                     nc.vector.tensor_scalar(y[:, a : a + m], banks[bank][:, c : c + m], bias[:, e : e + 1], 0.0, ADD, MAX)
                 else:
                     nc.scalar.activation(y[:, a : a + m], banks[bank][:, c : c + m], RELU, bias=bias[:, e : e + 1])

@@ -35,8 +35,8 @@ PIECES = (
     ((10, 2176, 512, 5, 0), (11, 2688, 128, 6, 0)),
     ((11, 2816, 128, 7, 0), (11, 2944, 128, 0, 0)),
 )
-PE_SUMS = ((0, 128), (128, 256))
-VECTOR_SUMS = ((384, 576), (960, 352), (1312, 224))
+PE_SUMS = (((0, 128),), ((128, 256),), ((384, 256), (640, 128)))
+VECTOR_SUMS = ((768, 288), (1056, 256), (1312, 224))
 
 
 def widths(slots):
@@ -148,11 +148,8 @@ def tile_moe_rag_lin_relu_kernel(tc, xT, w_words, w_scales, b, gate, offs, pos1,
             cols = slice(t0, t0 + n)
             nc.vector.tensor_tensor(dst[:, cols], y[:].indirect(pos[:, t0 // 16 : (t0 + n) // 16]), gates[:, choice, cols], MULT)
 
-        product(first, p1, 0, 0, VECTOR_SUMS[0][0])
-        product(second, p2, 1, 0, VECTOR_SUMS[0][0])
-        for i, (t0, n) in enumerate(PE_SUMS):
+        def turned_sum(t0, n, there, back):
             cols = slice(t0, t0 + n)
-            there, back = banks[2 * i], banks[2 * i + 1]
             for d in range(0, n, P):
                 block = slice(t0 + d, t0 + d + P)
                 nc.tensor.matmul(there[:, d : d + P], first[:, block], ident[:], start=True, stop=False, is_transpose=True)
@@ -162,6 +159,15 @@ def tile_moe_rag_lin_relu_kernel(tc, xT, w_words, w_scales, b, gate, offs, pos1,
                 nc.tensor.transpose(back[:, d : d + P], turned[:, t0 + d : t0 + d + P], ident[:])
             nc.scalar.copy(total[:, cols], back[:, :n])
             nc.sync.dma_start(out=out[:, cols], in_=total[:, cols])
+
+        free_banks = list(banks)
+        for groups in PE_SUMS:
+            t0 = groups[0][0]
+            n = sum(m for c, m in groups)
+            product(first, p1, 0, t0, n)
+            product(second, p2, 1, t0, n)
+            for c, m in groups:
+                turned_sum(c, m, free_banks.pop(0), free_banks.pop(0))
         product(first, p1, 0, VECTOR_SUMS[0][0], T - VECTOR_SUMS[0][0])
         for i in range(len(VECTOR_SUMS) + 1):
             if i < len(VECTOR_SUMS):

@@ -35,8 +35,8 @@ PIECES = (
     ((10, 2176, 512, 5, 0), (11, 2688, 128, 6, 0)),
     ((11, 2816, 128, 7, 0), (11, 2944, 128, 0, 0)),
 )
-PE_SUMS = (((0, 128),), ((128, 256),), ((384, 256), (640, 128)))
-VECTOR_SUMS = ((768, 288), (1056, 256), (1312, 224))
+PE_SUMS = (((0, 128), (128, 256), (384, 128)),)
+VECTOR_SUMS = ((512, 448), (960, 352), (1312, 224))
 
 
 def widths(slots):
@@ -158,7 +158,6 @@ def tile_moe_rag_lin_relu_kernel(tc, xT, w_words, w_scales, b, gate, offs, pos1,
             for d in range(0, n, P):
                 nc.tensor.transpose(back[:, d : d + P], turned[:, t0 + d : t0 + d + P], ident[:])
             nc.scalar.copy(total[:, cols], back[:, :n])
-            nc.sync.dma_start(out=out[:, cols], in_=total[:, cols])
 
         free_banks = list(banks)
         for groups in PE_SUMS:
@@ -168,6 +167,7 @@ def tile_moe_rag_lin_relu_kernel(tc, xT, w_words, w_scales, b, gate, offs, pos1,
             product(second, p2, 1, t0, n)
             for c, m in groups:
                 turned_sum(c, m, free_banks.pop(0), free_banks.pop(0))
+            nc.scalar.dma_start(out=out[:, t0 : t0 + n], in_=total[:, t0 : t0 + n])
         product(first, p1, 0, VECTOR_SUMS[0][0], T - VECTOR_SUMS[0][0])
         for i in range(len(VECTOR_SUMS) + 1):
             if i < len(VECTOR_SUMS):

@@ -35,8 +35,8 @@ PIECES = (
     ((10, 2176, 512, 5, 0), (11, 2688, 128, 6, 0)),
     ((11, 2816, 128, 7, 0), (11, 2944, 128, 0, 0)),
 )
-PE_SUMS = (((0, 128), (128, 256), (384, 128)),)
-VECTOR_SUMS = ((512, 448), (960, 352), (1312, 224))
+PE_SUMS = (((0, 128), (128, 128)), ((256, 256), (512, 128)))
+VECTOR_SUMS = ((640, 384), (1024, 320), (1344, 192))
 
 
 def widths(slots):

@@ -26,17 +26,19 @@ FLOPS = 2 * S * K * N
 
 LOADS = ((0, 1024), (1024, 256), (1280, 256))
 CHUNKS = ((0, 512, 304), (512, 512, 304), (1024, 256, 144), (1280, 256, 160))
-CODE_GATHERS = ((0, 1024), (1024, 1152), (2176, 640), (2816, 256))
-SCALE_GATHERS = CODE_GATHERS
-PIECES = (
-    ((0, 0, 128, 0, 0), (1, 128, 128, 0, 128), (2, 256, 128, 0, 256), (3, 384, 128, 0, 384),
-     (4, 512, 384, 1, 0), (5, 896, 128, 1, 384)),
-    ((6, 1024, 256, 2, 0), (8, 1792, 128, 2, 256), (7, 1280, 512, 3, 0), (9, 1920, 256, 4, 0)),
-    ((10, 2176, 512, 5, 0), (11, 2688, 128, 6, 0)),
-    ((11, 2816, 128, 7, 0), (11, 2944, 128, 0, 0)),
+WINDOW = 2048
+GATHERS = (
+    ("scales", 0, 1536, ()),
+    ("codes", 0, 1536, ((0, 0, 128, 0, 0), (1, 128, 128, 0, 128), (2, 256, 128, 0, 256), (3, 384, 128, 0, 384),
+                        (4, 512, 384, 1, 0), (5, 896, 128, 1, 384), (6, 1024, 256, 2, 0), (7, 1280, 256, 2, 256))),
+    ("scales", 1536, 1280, ()),
+    ("codes", 1536, 640, ((7, 1536, 256, 3, 0), (9, 1920, 256, 3, 256), (8, 1792, 128, 4, 0))),
+    ("codes", 2176, 640, ((10, 2176, 512, 5, 0), (11, 2688, 128, 6, 0))),
+    ("codes", 2816, 256, ()),
+    ("scales", 2816, 256, ((11, 2816, 128, 7, 0), (11, 2944, 128, 0, 0))),
 )
 PE_SUMS = (((0, 128), (128, 128)), ((256, 256), (512, 128)))
-VECTOR_SUMS = ((640, 384), (1024, 320), (1344, 192))
+VECTOR_SUMS = ((640, 512), (1152, 256), (1408, 128))
 
 
 def widths(slots):
@@ -54,8 +56,8 @@ def tile_moe_rag_lin_relu_kernel(tc, xT, w_words, w_scales, b, gate, offs, pos1,
         p1 = lists.tile([P, T // 16], U16, name="p1")
         p2 = lists.tile([P, T // 16], U16, name="p2")
 
-        codes = keep.tile([P, T], U32, name="codes", align_bytes=64)
-        scales = keep.tile([P, T], U8, name="scales", align_bytes=64)
+        codes = keep.tile([P, WINDOW], U32, name="codes", align_bytes=64)
+        scales = keep.tile([P, WINDOW], U8, name="scales", align_bytes=64)
         slot_codes = keep.tile([P, S], U32, name="slot_codes", align_bytes=64)
         slot_scales = keep.tile([P, S], U8, name="slot_scales", align_bytes=64)
         wt = keep.tile([P, E, 2 * N], U8, name="wt", align_bytes=64)
@@ -75,6 +77,8 @@ def tile_moe_rag_lin_relu_kernel(tc, xT, w_words, w_scales, b, gate, offs, pos1,
         make_identity(nc, ident[:])
         turned = keep.tile([P, T], F32, name="turned")
         nc.vector.memset(wt_scales[:].rearrange("p e n -> p (e n)").bitcast(I32), 0)
+
+        nc.vector.memset(codes[:, T:].bitcast(I32), 0)
 
         rows = xT.rearrange("(p j) t -> p j t", j=PACK)
         raw = []
@@ -120,12 +124,10 @@ def tile_moe_rag_lin_relu_kernel(tc, xT, w_words, w_scales, b, gate, offs, pos1,
         quantize(len(CHUNKS) - 1)
 
         banks = [psum.tile([P, 512], F32, name=f"bank{i}") for i in range(8)]
-        for gi, (s0, n) in enumerate(SCALE_GATHERS):
-            if gi < len(CODE_GATHERS):
-                c0, m = CODE_GATHERS[gi]
-                nc.vector.tensor_copy(slot_codes[:, c0 : c0 + m], codes[:].indirect(idx[:, c0 // 16 : (c0 + m) // 16]))
-            nc.vector.tensor_copy(slot_scales[:, s0 : s0 + n], scales[:].indirect(idx[:, s0 // 16 : (s0 + n) // 16]))
-            for e, a, m, bank, c in PIECES[gi]:
+        for sort, s0, n, runs in GATHERS:
+            src, dst = (codes, slot_codes) if sort == "codes" else (scales, slot_scales)
+            nc.vector.tensor_copy(dst[:, s0 : s0 + n], src[:].indirect(idx[:, s0 // 16 : (s0 + n) // 16]))
+            for e, a, m, bank, c in runs:
                 d = 0
                 for w in widths(m):
                     nc.tensor.matmul_mx(
@@ -138,7 +140,7 @@ def tile_moe_rag_lin_relu_kernel(tc, xT, w_words, w_scales, b, gate, offs, pos1,
                         stop=True,
                     )
                     d += w
-            for e, a, m, bank, c in PIECES[gi]:
+            for e, a, m, bank, c in runs:
                 if a + m == S - P:
                     nc.vector.tensor_scalar(y[:, a : a + m], banks[bank][:, c : c + m], bias[:, e : e + 1], 0.0, ADD, MAX)
                 else:

@@ -24,8 +24,12 @@ MULT = mybir.AluOpType.mult
 
 FLOPS = 2 * S * K * N
 
-LOADS = ((0, 1024), (1024, 256), (1280, 256))
-CHUNKS = ((0, 512, 304), (512, 512, 304), (1024, 256, 144), (1280, 256, 160))
+LOADS = ((0, 768), (768, 512), (1280, 256))
+HEAD = (
+    ("scalar", 0, 192), ("vector", 192, 384), ("scalar", 576, 192), ("quantise", 0, 512), ("quantise", 512, 256),
+    ("vector", 768, 256), ("vector", 1024, 48), ("scalar", 1072, 208), ("quantise", 768, 256),
+    ("vector", 1280, 128), ("scalar", 1408, 128), ("quantise", 1024, 256), ("quantise", 1280, 256),
+)
 WINDOW = 2048
 GATHERS = (
     ("scales", 0, 1536, ()),
@@ -85,7 +89,7 @@ def tile_moe_rag_lin_relu_kernel(tc, xT, w_words, w_scales, b, gate, offs, pos1,
         for i, (t0, n) in enumerate(LOADS):
             r = keep.tile([P, PACK, n], F32, name=f"raw{i}")
             nc.sync.dma_start(out=r[:], in_=rows[:, :, t0 : t0 + n])
-            raw += [(r, c0 - t0) for c0, m, v in CHUNKS if t0 <= c0 < t0 + n]
+            raw.append(r)
         nc.sync.dma_start(idx[:], offs)
         w_scales_i = w_scales.bitcast(I32)
         for q in range(4):
@@ -99,29 +103,22 @@ def tile_moe_rag_lin_relu_kernel(tc, xT, w_words, w_scales, b, gate, offs, pos1,
         nc.sync.dma_start(p2[:], pos2)
         nc.sync.dma_start(out=gates[:], in_=gate.rearrange("c p t -> p c t"))
 
-        grouped = []
-
-        def quantize(i):
-            t0, n, v = CHUNKS[i]
-            nc.vector.quantize_mx(
-                out=codes[:, t0 : t0 + n].bitcast(E4M3X4),
-                scales=scales[:, t0 : t0 + n],
-                in_=grouped[i][:].rearrange("p t j -> p (t j)"),
-            )
-
-        for i, (t0, n, v) in enumerate(CHUNKS):
-            r, c = raw[i]
-            g = keep.tile([P, n, PACK], BF16, name=f"grouped{i}", align_bytes=64)
-            nc.vector.tensor_copy(
-                g[:, :v, :].rearrange("p (q i) j -> p q j i", i=4), r[:, :, c : c + v].rearrange("p j (q i) -> p q j i", i=4)
-            )
-            nc.scalar.copy(
-                g[:, v:, :].rearrange("p (q i) j -> p q j i", i=4), r[:, :, c + v : c + n].rearrange("p j (q i) -> p q j i", i=4)
-            )
-            grouped.append(g)
-            if i > 0:
-                quantize(i - 1)
-        quantize(len(CHUNKS) - 1)
+        grouped = keep.tile([P, T, PACK], BF16, name="grouped", align_bytes=64)
+        for step, t0, n in HEAD:
+            if step == "quantise":
+                nc.vector.quantize_mx(
+                    out=codes[:, t0 : t0 + n].bitcast(E4M3X4),
+                    scales=scales[:, t0 : t0 + n],
+                    in_=grouped[:, t0 : t0 + n, :].rearrange("p t j -> p (t j)"),
+                )
+            else:
+                i = max(i for i, (c0, m) in enumerate(LOADS) if c0 <= t0)
+                c = t0 - LOADS[i][0]
+                copy = nc.vector.tensor_copy if step == "vector" else nc.scalar.copy
+                copy(
+                    grouped[:, t0 : t0 + n, :].rearrange("p (q i) j -> p q j i", i=4),
+                    raw[i][:, :, c : c + n].rearrange("p j (q i) -> p q j i", i=4),
+                )
 
         banks = [psum.tile([P, 512], F32, name=f"bank{i}") for i in range(8)]
         for sort, s0, n, runs in GATHERS:

@@ -41,8 +41,8 @@ GATHERS = (
     ("codes", 2816, 256, ()),
     ("scales", 2816, 256, ((11, 2816, 128, 7, 0), (11, 2944, 128, 0, 0))),
 )
-PE_SUMS = (((0, 128), (128, 128)), ((256, 256), (512, 128)))
-VECTOR_SUMS = ((640, 512), (1152, 256), (1408, 128))
+PE_SUMS = (((0, 256), (256, 256)),)
+VECTOR_SUMS = ((512, 704), (1216, 192), (1408, 128))
 
 
 def widths(slots):
@@ -167,12 +167,18 @@ def tile_moe_rag_lin_relu_kernel(tc, xT, w_words, w_scales, b, gate, offs, pos1,
             for c, m in groups:
                 turned_sum(c, m, free_banks.pop(0), free_banks.pop(0))
             nc.scalar.dma_start(out=out[:, t0 : t0 + n], in_=total[:, t0 : t0 + n])
-        product(first, p1, 0, VECTOR_SUMS[0][0], T - VECTOR_SUMS[0][0])
-        for i in range(len(VECTOR_SUMS) + 1):
-            if i < len(VECTOR_SUMS):
-                product(second, p2, 1, *VECTOR_SUMS[i])
-            if i > 0:
-                t0, n = VECTOR_SUMS[i - 1]
-                cols = slice(t0, t0 + n)
-                nc.vector.tensor_tensor(total[:, cols], first[:, cols], second[:, cols], ADD)
-                nc.sync.dma_start(out=out[:, cols], in_=total[:, cols])
+
+        def vector_sum(t0, n):
+            cols = slice(t0, t0 + n)
+            nc.vector.tensor_tensor(total[:, cols], first[:, cols], second[:, cols], ADD)
+            nc.sync.dma_start(out=out[:, cols], in_=total[:, cols])
+
+        large, middle, last = VECTOR_SUMS
+        product(first, p1, 0, *large)
+        product(second, p2, 1, *large)
+        product(first, p1, 0, middle[0], middle[1] + last[1])
+        vector_sum(*large)
+        product(second, p2, 1, *middle)
+        product(second, p2, 1, *last)
+        vector_sum(*middle)
+        vector_sum(*last)

@@ -41,8 +41,8 @@ GATHERS = (
     ("codes", 2816, 256, ()),
     ("scales", 2816, 256, ((11, 2816, 128, 7, 0), (11, 2944, 128, 0, 0))),
 )
-PE_SUMS = (((0, 256), (256, 256)),)
-VECTOR_SUMS = ((512, 704), (1216, 192), (1408, 128))
+PE_TOKENS = 640
+VECTOR_SUMS = ((640, 576), (1216, 192), (1408, 128))
 
 
 def widths(slots):
@@ -147,26 +147,25 @@ def tile_moe_rag_lin_relu_kernel(tc, xT, w_words, w_scales, b, gate, offs, pos1,
             cols = slice(t0, t0 + n)
             nc.vector.tensor_tensor(dst[:, cols], y[:].indirect(pos[:, t0 // 16 : (t0 + n) // 16]), gates[:, choice, cols], MULT)
 
-        def turned_sum(t0, n, there, back):
-            cols = slice(t0, t0 + n)
-            for d in range(0, n, P):
-                block = slice(t0 + d, t0 + d + P)
-                nc.tensor.matmul(there[:, d : d + P], first[:, block], ident[:], start=True, stop=False, is_transpose=True)
-                nc.tensor.matmul(there[:, d : d + P], second[:, block], ident[:], start=False, stop=True, is_transpose=True)
-            nc.scalar.copy(turned[:, cols], there[:, :n])
-            for d in range(0, n, P):
-                nc.tensor.transpose(back[:, d : d + P], turned[:, t0 + d : t0 + d + P], ident[:])
-            nc.scalar.copy(total[:, cols], back[:, :n])
-
-        free_banks = list(banks)
-        for groups in PE_SUMS:
-            t0 = groups[0][0]
-            n = sum(m for c, m in groups)
-            product(first, p1, 0, t0, n)
-            product(second, p2, 1, t0, n)
-            for c, m in groups:
-                turned_sum(c, m, free_banks.pop(0), free_banks.pop(0))
-            nc.scalar.dma_start(out=out[:, t0 : t0 + n], in_=total[:, t0 : t0 + n])
+        groups = [range(t0, min(t0 + 2 * P, PE_TOKENS), P) for t0 in range(0, PE_TOKENS, 2 * P)]
+        product(first, p1, 0, 0, PE_TOKENS)
+        for i, group in enumerate(groups):
+            for d, t0 in enumerate(group):
+                nc.tensor.matmul(banks[i][:, d * P : (d + 1) * P], first[:, t0 : t0 + P], ident[:], start=d == 0, stop=False, is_transpose=True)
+        product(second, p2, 1, 0, PE_TOKENS)
+        for i, group in enumerate(groups):
+            for d, t0 in enumerate(group):
+                nc.tensor.matmul(banks[i][:, d * P : (d + 1) * P], second[:, t0 : t0 + P], ident[:], start=False, stop=t0 == group[-1], is_transpose=True)
+            nc.scalar.copy(turned[:, group.start : group.stop], banks[i][:, : len(group) * P])
+        stored = 0
+        for i, group in enumerate(groups):
+            back = banks[len(groups) + i]
+            for d, t0 in enumerate(group):
+                nc.tensor.transpose(back[:, d * P : (d + 1) * P], turned[:, t0 : t0 + P], ident[:])
+            nc.scalar.copy(total[:, group.start : group.stop], back[:, : len(group) * P])
+            if i > 0:
+                nc.scalar.dma_start(out=out[:, stored : group.stop], in_=total[:, stored : group.stop])
+                stored = group.stop
 
         def vector_sum(t0, n):
             cols = slice(t0, t0 + n)

@@ -124,6 +124,17 @@ def tile_moe_rag_lin_relu_kernel(tc, xT, w_words, w_scales, b, gate, offs, pos1,
         for sort, s0, n, runs in GATHERS:
             src, dst = (codes, slot_codes) if sort == "codes" else (scales, slot_scales)
             nc.vector.tensor_copy(dst[:, s0 : s0 + n], src[:].indirect(idx[:, s0 // 16 : (s0 + n) // 16]))
+            if sort == "scales" and s0 == T:
+                for w in (512, 256):
+                    nc.tensor.matmul_mx(
+                        out=banks[7][:, :w],
+                        lhsT=wt[:, 0, :].bitcast(E2M1X4),
+                        lhsT_scale=wt_scales[:, 0, :],
+                        rhs=slot_codes[:, :w].bitcast(E4M3X4),
+                        rhs_scale=slot_scales[:, T : T + w],
+                        start=True,
+                        stop=True,
+                    )
             for e, a, m, bank, c in runs:
                 d = 0
                 for w in widths(m):

@@ -24,11 +24,12 @@ MULT = mybir.AluOpType.mult
 
 FLOPS = 2 * S * K * N
 
-LOADS = ((0, 768), (768, 512), (1280, 256))
+LOADS = ((0, 896), (896, 512), (1408, 128))
 HEAD = (
-    ("scalar", 0, 192), ("vector", 192, 384), ("scalar", 576, 192), ("quantise", 0, 512), ("quantise", 512, 256),
-    ("vector", 768, 256), ("vector", 1024, 48), ("scalar", 1072, 208), ("quantise", 768, 256),
-    ("vector", 1280, 128), ("scalar", 1408, 128), ("quantise", 1024, 256), ("quantise", 1280, 256),
+    ("scalar", 0, 192), ("vector", 192, 320), ("vector", 512, 192), ("scalar", 704, 192),
+    ("quantise", 0, 512), ("quantise", 512, 256), ("quantise", 768, 128),
+    ("vector", 896, 256), ("vector", 1152, 48), ("scalar", 1200, 208), ("quantise", 896, 256),
+    ("vector", 1408, 64), ("scalar", 1472, 64), ("quantise", 1152, 256), ("quantise", 1408, 128),
 )
 WINDOW = 2048
 GATHERS = (
@@ -41,8 +42,8 @@ GATHERS = (
     ("codes", 2816, 256, ()),
     ("scales", 2816, 256, ((11, 2816, 128, 7, 0), (11, 2944, 128, 0, 0))),
 )
-PE_TOKENS = 640
-VECTOR_SUMS = ((640, 576), (1216, 192), (1408, 128))
+PE_GROUPS = ((0, 256), (256, 256), (512, 128), (640, 128))
+VECTOR_SUMS = ((768, 448), (1216, 192), (1408, 128))
 
 
 def widths(slots):
@@ -158,23 +159,35 @@ def tile_moe_rag_lin_relu_kernel(tc, xT, w_words, w_scales, b, gate, offs, pos1,
             cols = slice(t0, t0 + n)
             nc.vector.tensor_tensor(dst[:, cols], y[:].indirect(pos[:, t0 // 16 : (t0 + n) // 16]), gates[:, choice, cols], MULT)
 
-        groups = [range(t0, min(t0 + 2 * P, PE_TOKENS), P) for t0 in range(0, PE_TOKENS, 2 * P)]
-        product(first, p1, 0, 0, PE_TOKENS)
-        for i, group in enumerate(groups):
-            for d, t0 in enumerate(group):
-                nc.tensor.matmul(banks[i][:, d * P : (d + 1) * P], first[:, t0 : t0 + P], ident[:], start=d == 0, stop=False, is_transpose=True)
-        product(second, p2, 1, 0, PE_TOKENS)
-        for i, group in enumerate(groups):
-            for d, t0 in enumerate(group):
-                nc.tensor.matmul(banks[i][:, d * P : (d + 1) * P], second[:, t0 : t0 + P], ident[:], start=False, stop=t0 == group[-1], is_transpose=True)
+        def turn(src, group, bank, blocks, opens, closes):
+            for t0 in blocks:
+                d = t0 - group.start
+                nc.tensor.matmul(
+                    bank[:, d : d + P], src[:, t0 : t0 + P], ident[:],
+                    start=opens and t0 == group[0], stop=closes and t0 == group[-1], is_transpose=True,
+                )
+
+        groups = [range(t0, t0 + n, P) for t0, n in PE_GROUPS]
+        early, late = groups[:-1], groups[-1]
+        large, middle, last = VECTOR_SUMS
+        product(first, p1, 0, 0, late.start)
+        for i, group in enumerate(early):
+            turn(first, group, banks[i], group, True, False)
+        product(second, p2, 1, 0, late.stop)
+        for i, group in enumerate(early):
+            turn(second, group, banks[i], group, False, True)
             nc.scalar.copy(turned[:, group.start : group.stop], banks[i][:, : len(group) * P])
+        turn(second, late, banks[len(early)], late, True, False)
+        product(first, p1, 0, late.start, len(late) * P + large[1])
+        turn(first, late, banks[len(early)], late, False, True)
+        nc.scalar.copy(turned[:, late.start : late.stop], banks[len(early)][:, : len(late) * P])
         stored = 0
         for i, group in enumerate(groups):
             back = banks[len(groups) + i]
             for d, t0 in enumerate(group):
                 nc.tensor.transpose(back[:, d * P : (d + 1) * P], turned[:, t0 : t0 + P], ident[:])
             nc.scalar.copy(total[:, group.start : group.stop], back[:, : len(group) * P])
-            if i > 0:
+            if i % 2 == 1:
                 nc.scalar.dma_start(out=out[:, stored : group.stop], in_=total[:, stored : group.stop])
                 stored = group.stop
 
@@ -183,8 +196,6 @@ def tile_moe_rag_lin_relu_kernel(tc, xT, w_words, w_scales, b, gate, offs, pos1,
             nc.vector.tensor_tensor(total[:, cols], first[:, cols], second[:, cols], ADD)
             nc.sync.dma_start(out=out[:, cols], in_=total[:, cols])
 
-        large, middle, last = VECTOR_SUMS
-        product(first, p1, 0, *large)
         product(second, p2, 1, *large)
         product(first, p1, 0, middle[0], middle[1] + last[1])
         vector_sum(*large)

@@ -1,7 +1,6 @@
 from contextlib import ExitStack
 
 import concourse.mybir as mybir
-from concourse.masks import make_identity
 
 K, T, E, N = 512, 1536, 12, 128
 COUNTS = (128, 128, 128, 128, 384, 128, 256, 512, 128, 256, 512, 384)
@@ -17,6 +16,7 @@ U16 = mybir.dt.uint16
 U8 = mybir.dt.uint8
 E4M3X4 = mybir.dt.float8_e4m3fn_x4
 E2M1X4 = mybir.dt.float4_e2m1fn_x4
+COPY = mybir.ActivationFunctionType.Copy
 RELU = mybir.ActivationFunctionType.Relu
 ADD = mybir.AluOpType.add
 MAX = mybir.AluOpType.max
@@ -42,8 +42,8 @@ GATHERS = (
     ("codes", 2816, 256, ()),
     ("scales", 2816, 256, ((11, 2816, 128, 7, 0), (11, 2944, 128, 0, 0))),
 )
-PE_GROUPS = ((0, 256), (256, 256), (512, 128), (640, 128))
-VECTOR_SUMS = ((768, 448), (1216, 192), (1408, 128))
+FUSED = 640
+PAIRED = (256, 256, 192, 128, 64)
 
 
 def widths(slots):
@@ -70,17 +70,14 @@ def tile_moe_rag_lin_relu_kernel(tc, xT, w_words, w_scales, b, gate, offs, pos1,
         bias = keep.tile([P, E], F32, name="bias")
         gates = keep.tile([P, 2, T], F32, name="gates")
         y = keep.tile([P, S], F32, name="y")
-        first = keep.tile([P, T], F32, name="first")
-        second = keep.tile([P, T], F32, name="second")
+        fetched = keep.tile([P, 2, T], F32, name="fetched")
+        gated = keep.tile([P, 2, T], F32, name="gated")
         total = keep.tile([P, T], F32, name="total")
         warm = keep.tile([P, 1], F32, name="warm")
 
         nc.gpsimd.memset(warm[:], 0.0)
         nc.scalar.activation(warm[:], warm[:], RELU)
         nc.gpsimd.memset(scales[:], 0)
-        ident = keep.tile([P, P], F32, name="ident")
-        make_identity(nc, ident[:])
-        turned = keep.tile([P, T], F32, name="turned")
         nc.vector.memset(wt_scales[:].rearrange("p e n -> p (e n)").bitcast(I32), 0)
 
         nc.vector.memset(codes[:, T:].bitcast(I32), 0)
@@ -125,17 +122,6 @@ def tile_moe_rag_lin_relu_kernel(tc, xT, w_words, w_scales, b, gate, offs, pos1,
         for sort, s0, n, runs in GATHERS:
             src, dst = (codes, slot_codes) if sort == "codes" else (scales, slot_scales)
             nc.vector.tensor_copy(dst[:, s0 : s0 + n], src[:].indirect(idx[:, s0 // 16 : (s0 + n) // 16]))
-            if sort == "scales" and s0 == T:
-                for w in (512, 256):
-                    nc.tensor.matmul_mx(
-                        out=banks[7][:, :w],
-                        lhsT=wt[:, 0, :].bitcast(E2M1X4),
-                        lhsT_scale=wt_scales[:, 0, :],
-                        rhs=slot_codes[:, :w].bitcast(E4M3X4),
-                        rhs_scale=slot_scales[:, T : T + w],
-                        start=True,
-                        stop=True,
-                    )
             for e, a, m, bank, c in runs:
                 d = 0
                 for w in widths(m):
@@ -155,51 +141,32 @@ def tile_moe_rag_lin_relu_kernel(tc, xT, w_words, w_scales, b, gate, offs, pos1,
                 else:
                     nc.scalar.activation(y[:, a : a + m], banks[bank][:, c : c + m], RELU, bias=bias[:, e : e + 1])
 
-        def product(dst, pos, choice, t0, n):
+        pos = (p1, p2)
+
+        def entries(choice, t0, n):
+            return y[:].indirect(pos[choice][:, t0 // 16 : (t0 + n) // 16])
+
+        def fetch(choice, t0, n):
+            nc.scalar.activation(fetched[:, choice, t0 : t0 + n], entries(choice, t0, n), COPY)
+
+        def weigh(choices, t0, n):
+            nc.vector.tensor_tensor(gated[:, choices, t0 : t0 + n], fetched[:, choices, t0 : t0 + n], gates[:, choices, t0 : t0 + n], MULT)
+
+        def add_and_store(t0, n):
             cols = slice(t0, t0 + n)
-            nc.vector.tensor_tensor(dst[:, cols], y[:].indirect(pos[:, t0 // 16 : (t0 + n) // 16]), gates[:, choice, cols], MULT)
-
-        def turn(src, group, bank, blocks, opens, closes):
-            for t0 in blocks:
-                d = t0 - group.start
-                nc.tensor.matmul(
-                    bank[:, d : d + P], src[:, t0 : t0 + P], ident[:],
-                    start=opens and t0 == group[0], stop=closes and t0 == group[-1], is_transpose=True,
-                )
-
-        groups = [range(t0, t0 + n, P) for t0, n in PE_GROUPS]
-        early, late = groups[:-1], groups[-1]
-        large, middle, last = VECTOR_SUMS
-        product(first, p1, 0, 0, late.start)
-        for i, group in enumerate(early):
-            turn(first, group, banks[i], group, True, False)
-        product(second, p2, 1, 0, late.stop)
-        for i, group in enumerate(early):
-            turn(second, group, banks[i], group, False, True)
-            nc.scalar.copy(turned[:, group.start : group.stop], banks[i][:, : len(group) * P])
-        turn(second, late, banks[len(early)], late, True, False)
-        product(first, p1, 0, late.start, len(late) * P + large[1])
-        turn(first, late, banks[len(early)], late, False, True)
-        nc.scalar.copy(turned[:, late.start : late.stop], banks[len(early)][:, : len(late) * P])
-        stored = 0
-        for i, group in enumerate(groups):
-            back = banks[len(groups) + i]
-            for d, t0 in enumerate(group):
-                nc.tensor.transpose(back[:, d * P : (d + 1) * P], turned[:, t0 : t0 + P], ident[:])
-            nc.scalar.copy(total[:, group.start : group.stop], back[:, : len(group) * P])
-            if i % 2 == 1:
-                nc.scalar.dma_start(out=out[:, stored : group.stop], in_=total[:, stored : group.stop])
-                stored = group.stop
-
-        def vector_sum(t0, n):
-            cols = slice(t0, t0 + n)
-            nc.vector.tensor_tensor(total[:, cols], first[:, cols], second[:, cols], ADD)
+            nc.vector.tensor_tensor(total[:, cols], gated[:, 0, cols], gated[:, 1, cols], ADD)
             nc.sync.dma_start(out=out[:, cols], in_=total[:, cols])
 
-        product(second, p2, 1, *large)
-        product(first, p1, 0, middle[0], middle[1] + last[1])
-        vector_sum(*large)
-        product(second, p2, 1, *middle)
-        product(second, p2, 1, *last)
-        vector_sum(*middle)
-        vector_sum(*last)
+        nc.vector.tensor_tensor(gated[:, 0, :FUSED], entries(0, 0, FUSED), gates[:, 0, :FUSED], MULT)
+        fetch(1, 0, FUSED)
+        weigh(slice(1, 2), 0, FUSED)
+        waiting = (0, FUSED)
+        t0 = FUSED
+        for n in PAIRED:
+            fetch(0, t0, n)
+            fetch(1, t0, n)
+            weigh(slice(0, 2), t0, n)
+            add_and_store(*waiting)
+            waiting = (t0, n)
+            t0 += n
+        add_and_store(*waiting)

@@ -42,8 +42,8 @@ GATHERS = (
     ("codes", 2816, 256, ()),
     ("scales", 2816, 256, ((11, 2816, 128, 7, 0), (11, 2944, 128, 0, 0))),
 )
-FUSED = 640
-PAIRED = (256, 256, 192, 128, 64)
+FUSED = (512, 448)
+PAIRED = (256, 192, 128)
 
 
 def widths(slots):
@@ -157,16 +157,17 @@ def tile_moe_rag_lin_relu_kernel(tc, xT, w_words, w_scales, b, gate, offs, pos1,
             nc.vector.tensor_tensor(total[:, cols], gated[:, 0, cols], gated[:, 1, cols], ADD)
             nc.sync.dma_start(out=out[:, cols], in_=total[:, cols])
 
-        nc.vector.tensor_tensor(gated[:, 0, :FUSED], entries(0, 0, FUSED), gates[:, 0, :FUSED], MULT)
-        fetch(1, 0, FUSED)
-        weigh(slice(1, 2), 0, FUSED)
-        waiting = (0, FUSED)
-        t0 = FUSED
-        for n in PAIRED:
-            fetch(0, t0, n)
-            fetch(1, t0, n)
-            weigh(slice(0, 2), t0, n)
-            add_and_store(*waiting)
+        fused = sum(FUSED)
+        nc.vector.tensor_tensor(gated[:, 0, :fused], entries(0, 0, fused), gates[:, 0, :fused], MULT)
+        waiting = None
+        t0 = 0
+        for n in FUSED + PAIRED:
+            first = 1 if t0 < fused else 0
+            for choice in range(first, 2):
+                fetch(choice, t0, n)
+            weigh(slice(first, 2), t0, n)
+            if waiting:
+                add_and_store(*waiting)
             waiting = (t0, n)
             t0 += n
         add_and_store(*waiting)

@@ -36,14 +36,14 @@ GATHERS = (
     ("scales", 0, 1536, ()),
     ("codes", 0, 1536, ((0, 0, 128, 0, 0), (1, 128, 128, 0, 128), (2, 256, 128, 0, 256), (3, 384, 128, 0, 384),
                         (4, 512, 384, 1, 0), (5, 896, 128, 1, 384), (6, 1024, 256, 2, 0), (7, 1280, 256, 2, 256))),
-    ("scales", 1536, 1280, ()),
+    ("scales", 1536, 1536, ()),
     ("codes", 1536, 640, ((7, 1536, 256, 3, 0), (9, 1920, 256, 3, 256), (8, 1792, 128, 4, 0))),
-    ("codes", 2176, 640, ((10, 2176, 512, 5, 0), (11, 2688, 128, 6, 0))),
-    ("codes", 2816, 256, ()),
-    ("scales", 2816, 256, ((11, 2816, 128, 7, 0), (11, 2944, 128, 0, 0))),
+    ("codes", 2176, 512, ((10, 2176, 256, 5, 0), (10, 2432, 256, 6, 0))),
+    ("codes", 2688, 256, ((11, 2688, 256, 7, 0),)),
+    ("codes", 2944, 128, ((11, 2944, 128, 0, 0),)),
 )
-FUSED = (512, 448)
-PAIRED = (256, 192, 128)
+FUSED = (512, 512)
+PAIRED = (256, 160, 96)
 
 
 def widths(slots):

@@ -34,10 +34,11 @@ HEAD = (
 WINDOW = 2048
 GATHERS = (
     ("scales", 0, 1536, ()),
-    ("codes", 0, 1536, ((0, 0, 128, 0, 0), (1, 128, 128, 0, 128), (2, 256, 128, 0, 256), (3, 384, 128, 0, 384),
-                        (4, 512, 384, 1, 0), (5, 896, 128, 1, 384), (6, 1024, 256, 2, 0), (7, 1280, 256, 2, 256))),
     ("scales", 1536, 1536, ()),
-    ("codes", 1536, 640, ((7, 1536, 256, 3, 0), (9, 1920, 256, 3, 256), (8, 1792, 128, 4, 0))),
+    ("codes", 0, 1024, ((0, 0, 128, 0, 0), (1, 128, 128, 0, 128), (2, 256, 128, 0, 256), (3, 384, 128, 0, 384),
+                        (4, 512, 384, 1, 0), (5, 896, 128, 1, 384))),
+    ("codes", 1024, 768, ((6, 1024, 256, 2, 0), (7, 1280, 512, 3, 0))),
+    ("codes", 1792, 384, ((8, 1792, 128, 4, 0), (9, 1920, 256, 4, 128))),
     ("codes", 2176, 512, ((10, 2176, 256, 5, 0), (10, 2432, 256, 6, 0))),
     ("codes", 2688, 256, ((11, 2688, 256, 7, 0),)),
     ("codes", 2944, 128, ((11, 2944, 128, 0, 0),)),

@@ -115,8 +115,8 @@ def tile_moe_rag_lin_relu_kernel(tc, xT, w_words, w_scales, b, gate, offs, pos1,
                 c = t0 - LOADS[i][0]
                 copy = nc.vector.tensor_copy if step == "vector" else nc.scalar.copy
                 copy(
-                    grouped[:, t0 : t0 + n, :].rearrange("p (q i) j -> p q j i", i=4),
-                    raw[i][:, :, c : c + n].rearrange("p j (q i) -> p q j i", i=4),
+                    grouped[:, t0 : t0 + n, :].rearrange("p (q i) j -> p q j i", i=2),
+                    raw[i][:, :, c : c + n].rearrange("p j (q i) -> p q j i", i=2),
                 )
 
         banks = [psum.tile([P, 512], F32, name=f"bank{i}") for i in range(8)]

@@ -3,11 +3,12 @@ from contextlib import ExitStack
 import concourse.mybir as mybir
 
 K, T, E, N = 512, 1536, 12, 128
-COUNTS = (128, 128, 128, 128, 384, 128, 256, 512, 128, 256, 512, 384)
-S = 3072
+S = 2 * T
 
 P = 128
 PACK = 4
+PER_COLUMN = 16
+BANK = 512
 F32 = mybir.dt.float32
 BF16 = mybir.dt.bfloat16
 U32 = mybir.dt.uint32
@@ -31,24 +32,22 @@ HEAD = (
     ("vector", 896, 256), ("vector", 1152, 48), ("scalar", 1200, 208), ("quantise", 896, 256),
     ("vector", 1408, 64), ("scalar", 1472, 64), ("quantise", 1152, 256), ("quantise", 1408, 128),
 )
-WINDOW = 2048
-GATHERS = (
-    ("scales", 0, 1536, ()),
-    ("scales", 1536, 1536, ()),
-    ("codes", 0, 1024, ((0, 0, 128, 0, 0), (1, 128, 128, 0, 128), (2, 256, 128, 0, 256), (3, 384, 128, 0, 384),
-                        (4, 512, 384, 1, 0), (5, 896, 128, 1, 384))),
-    ("codes", 1024, 768, ((6, 1024, 256, 2, 0), (7, 1280, 512, 3, 0))),
-    ("codes", 1792, 384, ((8, 1792, 128, 4, 0), (9, 1920, 256, 4, 128))),
-    ("codes", 2176, 512, ((10, 2176, 256, 5, 0), (10, 2432, 256, 6, 0))),
-    ("codes", 2688, 256, ((11, 2688, 256, 7, 0),)),
-    ("codes", 2944, 128, ((11, 2944, 128, 0, 0),)),
+NEIGHBOURS = 2
+SCALE_COLUMNS = 2048
+BATCHES = (
+    ((0, 128, 0, 0), (1, 128, 0, 128), (2, 128, 0, 256), (3, 128, 0, 384), (4, 384, 1, 0), (5, 128, 1, 384)),
+    ((6, 256, 2, 0), (7, 512, 3, 0)),
+    ((8, 128, 4, 0), (9, 256, 4, 128)),
+    ((10, 256, 5, 0), (10, 256, 6, 0)),
+    ((11, 256, 7, 0),),
+    ((11, 128, 0, 0),),
 )
 FUSED = (512, 512)
 PAIRED = (256, 160, 96)
 
 
 def widths(slots):
-    return {128: (128,), 256: (256,), 384: (256, 128), 512: (512,)}[slots]
+    return (256, 128) if slots == 384 else (slots,)
 
 
 def tile_moe_rag_lin_relu_kernel(tc, xT, w_words, w_scales, b, gate, offs, pos1, pos2, out):
@@ -58,12 +57,12 @@ def tile_moe_rag_lin_relu_kernel(tc, xT, w_words, w_scales, b, gate, offs, pos1,
         keep = ctx.enter_context(tc.tile_pool(name="keep", bufs=1))
         psum = ctx.enter_context(tc.psum_pool(name="psum", bufs=1))
 
-        idx = lists.tile([P, 2 * T // 16], U16, name="idx")
-        p1 = lists.tile([P, T // 16], U16, name="p1")
-        p2 = lists.tile([P, T // 16], U16, name="p2")
+        idx = lists.tile([P, S // PER_COLUMN], U16, name="idx")
+        p1 = lists.tile([P, T // PER_COLUMN], U16, name="p1")
+        p2 = lists.tile([P, T // PER_COLUMN], U16, name="p2")
 
-        codes = keep.tile([P, WINDOW], U32, name="codes", align_bytes=64)
-        scales = keep.tile([P, WINDOW], U8, name="scales", align_bytes=64)
+        codes = keep.tile([P, T], U32, name="codes", align_bytes=64)
+        scales = keep.tile([P, SCALE_COLUMNS], U8, name="scales", align_bytes=64)
         slot_codes = keep.tile([P, S], U32, name="slot_codes", align_bytes=64)
         slot_scales = keep.tile([P, S], U8, name="slot_scales", align_bytes=64)
         wt = keep.tile([P, E, 2 * N], U8, name="wt", align_bytes=64)
@@ -80,8 +79,6 @@ def tile_moe_rag_lin_relu_kernel(tc, xT, w_words, w_scales, b, gate, offs, pos1,
         nc.scalar.activation(warm[:], warm[:], RELU)
         nc.gpsimd.memset(scales[:], 0)
         nc.vector.memset(wt_scales[:].rearrange("p e n -> p (e n)").bitcast(I32), 0)
-
-        nc.vector.memset(codes[:, T:].bitcast(I32), 0)
 
         rows = xT.rearrange("(p j) t -> p j t", j=PACK)
         raw = []
@@ -111,33 +108,41 @@ def tile_moe_rag_lin_relu_kernel(tc, xT, w_words, w_scales, b, gate, offs, pos1,
                     in_=grouped[:, t0 : t0 + n, :].rearrange("p t j -> p (t j)"),
                 )
             else:
-                i = max(i for i, (c0, m) in enumerate(LOADS) if c0 <= t0)
-                c = t0 - LOADS[i][0]
+                load = max(i for i, (first, count) in enumerate(LOADS) if first <= t0)
+                c = t0 - LOADS[load][0]
                 copy = nc.vector.tensor_copy if step == "vector" else nc.scalar.copy
                 copy(
-                    grouped[:, t0 : t0 + n, :].rearrange("p (q i) j -> p q j i", i=2),
-                    raw[i][:, :, c : c + n].rearrange("p j (q i) -> p q j i", i=2),
+                    grouped[:, t0 : t0 + n, :].rearrange("p (q i) j -> p q j i", i=NEIGHBOURS),
+                    raw[load][:, :, c : c + n].rearrange("p j (q i) -> p q j i", i=NEIGHBOURS),
                 )
 
-        banks = [psum.tile([P, 512], F32, name=f"bank{i}") for i in range(8)]
-        for sort, s0, n, runs in GATHERS:
-            src, dst = (codes, slot_codes) if sort == "codes" else (scales, slot_scales)
-            nc.vector.tensor_copy(dst[:, s0 : s0 + n], src[:].indirect(idx[:, s0 // 16 : (s0 + n) // 16]))
-            for e, a, m, bank, c in runs:
+        def gather_slots(dst, src, s0, n):
+            nc.vector.tensor_copy(dst[:, s0 : s0 + n], src[:].indirect(idx[:, s0 // PER_COLUMN : (s0 + n) // PER_COLUMN]))
+
+        banks = [psum.tile([P, BANK], F32, name=f"bank{i}") for i in range(8)]
+        for s0 in (0, S // 2):
+            gather_slots(slot_scales, scales, s0, S // 2)
+        s0 = 0
+        for batch in BATCHES:
+            gather_slots(slot_codes, codes, s0, sum(run[1] for run in batch))
+            starts = []
+            for e, m, bank, c in batch:
+                starts.append(s0)
                 d = 0
                 for w in widths(m):
                     nc.tensor.matmul_mx(
                         out=banks[bank][:, c + d : c + d + w],
                         lhsT=wt[:, e, :].bitcast(E2M1X4),
                         lhsT_scale=wt_scales[:, e, :],
-                        rhs=slot_codes[:, a + d : a + d + w].bitcast(E4M3X4),
-                        rhs_scale=slot_scales[:, a + d : a + d + w],
+                        rhs=slot_codes[:, s0 + d : s0 + d + w].bitcast(E4M3X4),
+                        rhs_scale=slot_scales[:, s0 + d : s0 + d + w],
                         start=True,
                         stop=True,
                     )
                     d += w
-            for e, a, m, bank, c in runs:
-                if a + m == S - P:
+                s0 += m
+            for a, (e, m, bank, c) in zip(starts, batch):
+                if batch == BATCHES[-2]:
                     nc.vector.tensor_scalar(y[:, a : a + m], banks[bank][:, c : c + m], bias[:, e : e + 1], 0.0, ADD, MAX)
                 else:
                     nc.scalar.activation(y[:, a : a + m], banks[bank][:, c : c + m], RELU, bias=bias[:, e : e + 1])
@@ -145,7 +150,7 @@ def tile_moe_rag_lin_relu_kernel(tc, xT, w_words, w_scales, b, gate, offs, pos1,
         pos = (p1, p2)
 
         def entries(choice, t0, n):
-            return y[:].indirect(pos[choice][:, t0 // 16 : (t0 + n) // 16])
+            return y[:].indirect(pos[choice][:, t0 // PER_COLUMN : (t0 + n) // PER_COLUMN])
 
         def fetch(choice, t0, n):
             nc.scalar.activation(fetched[:, choice, t0 : t0 + n], entries(choice, t0, n), COPY)

@@ -1,6 +1,7 @@
 from contextlib import ExitStack
 
 import concourse.mybir as mybir
+from concourse.masks import make_identity
 
 K, T, E, N = 512, 1536, 12, 128
 S = 2 * T
@@ -37,13 +38,14 @@ SCALE_COLUMNS = 2048
 BATCHES = (
     ((0, 128, 0, 0), (1, 128, 0, 128), (2, 128, 0, 256), (3, 128, 0, 384), (4, 384, 1, 0), (5, 128, 1, 384)),
     ((6, 256, 2, 0), (7, 512, 3, 0)),
-    ((8, 128, 4, 0), (9, 256, 4, 128)),
-    ((10, 256, 5, 0), (10, 256, 6, 0)),
-    ((11, 256, 7, 0),),
+    ((8, 128, 0, 0), (9, 256, 0, 128)),
+    ((10, 256, 1, 0), (10, 256, 2, 0)),
+    ((11, 256, 3, 0),),
     ((11, 128, 0, 0),),
 )
-FUSED = (512, 512)
-PAIRED = (256, 160, 96)
+FUSED = 1280
+FUSED_AHEAD = 896
+SUMS_ON_GPSIMD = (256, 256)
 
 
 def widths(slots):
@@ -68,7 +70,11 @@ def tile_moe_rag_lin_relu_kernel(tc, xT, w_words, w_scales, b, gate, offs, pos1,
         wt = keep.tile([P, E, 2 * N], U8, name="wt", align_bytes=64)
         wt_scales = keep.tile([P, E, N], U8, name="wt_scales", align_bytes=64)
         bias = keep.tile([P, E], F32, name="bias")
-        gates = keep.tile([P, 2, T], F32, name="gates")
+        gate0 = keep.tile([P, FUSED], F32, name="gate0")
+        gate_rows = keep.tile([P, P], F32, name="gate_rows")
+        blocks = (2 * T - FUSED) // P
+        gate_cols = keep.tile([P, blocks], F32, name="gate_cols")
+        identity = keep.tile([P, P], F32, name="identity")
         y = keep.tile([P, S], F32, name="y")
         fetched = keep.tile([P, 2, T], F32, name="fetched")
         gated = keep.tile([P, 2, T], F32, name="gated")
@@ -80,6 +86,9 @@ def tile_moe_rag_lin_relu_kernel(tc, xT, w_words, w_scales, b, gate, offs, pos1,
         nc.gpsimd.memset(scales[:], 0)
         nc.vector.memset(wt_scales[:].rearrange("p e n -> p (e n)").bitcast(I32), 0)
 
+        nc.gpsimd.memset(gate_rows[:], 0.0)
+        make_identity(nc, identity[:])
+
         rows = xT.rearrange("(p j) t -> p j t", j=PACK)
         raw = []
         for i, (t0, n) in enumerate(LOADS):
@@ -87,6 +96,8 @@ def tile_moe_rag_lin_relu_kernel(tc, xT, w_words, w_scales, b, gate, offs, pos1,
             nc.sync.dma_start(out=r[:], in_=rows[:, :, t0 : t0 + n])
             raw.append(r)
         nc.sync.dma_start(idx[:], offs)
+        flat = gate.rearrange("c n t -> (c n t)")
+        nc.sync.dma_start(out=gate_rows[:blocks, :], in_=flat[(N - 1) * T + FUSED : (N + 1) * T].rearrange("(r t) -> r t", t=P))
         w_scales_i = w_scales.bitcast(I32)
         for q in range(4):
             nc.sync.dma_start(
@@ -97,7 +108,7 @@ def tile_moe_rag_lin_relu_kernel(tc, xT, w_words, w_scales, b, gate, offs, pos1,
         nc.sync.dma_start(out=bias[:], in_=b)
         nc.sync.dma_start(p1[:], pos1)
         nc.sync.dma_start(p2[:], pos2)
-        nc.sync.dma_start(out=gates[:], in_=gate.rearrange("c p t -> p c t"))
+        nc.sync.dma_start(out=gate0[:], in_=gate[0, :, :FUSED])
 
         grouped = keep.tile([P, T, PACK], BF16, name="grouped", align_bytes=64)
         for step, t0, n in HEAD:
@@ -120,6 +131,12 @@ def tile_moe_rag_lin_relu_kernel(tc, xT, w_words, w_scales, b, gate, offs, pos1,
             nc.vector.tensor_copy(dst[:, s0 : s0 + n], src[:].indirect(idx[:, s0 // PER_COLUMN : (s0 + n) // PER_COLUMN]))
 
         banks = [psum.tile([P, BANK], F32, name=f"bank{i}") for i in range(8)]
+        order = [(1, t) for t in range(0, FUSED, P)] + [(c, t) for t in range(FUSED, T, P) for c in range(2)]
+        nc.tensor.transpose(banks[0][:, :P], gate_rows[:], identity[:])
+        nc.scalar.copy(gate_cols[:], banks[0][:, :blocks])
+        for i, (c, t) in enumerate(order):
+            r = (t - FUSED + c * T) // P
+            nc.tensor.transpose(banks[4 + i // 4][:, i % 4 * P : (i % 4 + 1) * P], gate_cols[:, r : r + 1].to_broadcast([P, P]), identity[:])
         for s0 in (0, S // 2):
             gather_slots(slot_scales, scales, s0, S // 2)
         s0 = 0
@@ -152,28 +169,40 @@ def tile_moe_rag_lin_relu_kernel(tc, xT, w_words, w_scales, b, gate, offs, pos1,
         def entries(choice, t0, n):
             return y[:].indirect(pos[choice][:, t0 // PER_COLUMN : (t0 + n) // PER_COLUMN])
 
-        def fetch(choice, t0, n):
-            nc.scalar.activation(fetched[:, choice, t0 : t0 + n], entries(choice, t0, n), COPY)
+        def fetch_and_weigh(t0, n):
+            first = 1 if t0 < FUSED else 0
+            for c in range(first, 2):
+                nc.scalar.activation(fetched[:, c, t0 : t0 + n], entries(c, t0, n), COPY)
+            i = order.index((first, t0))
+            gates = banks[4 + i // 4][:, i % 4 * P : i % 4 * P + (2 - first) * n].rearrange("p (c t) -> p c t", t=n)
+            nc.vector.tensor_tensor(gated[:, first:, t0 : t0 + n], fetched[:, first:, t0 : t0 + n], gates, MULT)
 
-        def weigh(choices, t0, n):
-            nc.vector.tensor_tensor(gated[:, choices, t0 : t0 + n], fetched[:, choices, t0 : t0 + n], gates[:, choices, t0 : t0 + n], MULT)
+        def fused(t0, t1):
+            nc.vector.tensor_tensor(gated[:, 0, t0:t1], entries(0, t0, t1 - t0), gate0[:, t0:t1], MULT)
 
-        def add_and_store(t0, n):
-            cols = slice(t0, t0 + n)
-            nc.vector.tensor_tensor(total[:, cols], gated[:, 0, cols], gated[:, 1, cols], ADD)
-            nc.sync.dma_start(out=out[:, cols], in_=total[:, cols])
+        def add(engine, t0, n):
+            engine.tensor_tensor(total[:, t0 : t0 + n], gated[:, 0, t0 : t0 + n], gated[:, 1, t0 : t0 + n], ADD)
 
-        fused = sum(FUSED)
-        nc.vector.tensor_tensor(gated[:, 0, :fused], entries(0, 0, fused), gates[:, 0, :fused], MULT)
-        waiting = None
+        def store(t0, n):
+            nc.sync.dma_start(out=out[:, t0 : t0 + n], in_=total[:, t0 : t0 + n])
+
+        fused(0, FUSED_AHEAD)
+        fetch_and_weigh(0, 512)
+        fused(FUSED_AHEAD, FUSED)
         t0 = 0
-        for n in FUSED + PAIRED:
-            first = 1 if t0 < fused else 0
-            for choice in range(first, 2):
-                fetch(choice, t0, n)
-            weigh(slice(first, 2), t0, n)
-            if waiting:
-                add_and_store(*waiting)
-            waiting = (t0, n)
+        for n in SUMS_ON_GPSIMD:
+            add(nc.gpsimd, t0, n)
+            store(t0, n)
             t0 += n
-        add_and_store(*waiting)
+        fetch_and_weigh(512, 512)
+        fetch_and_weigh(1024, 256)
+        fetch_and_weigh(1280, 128)
+        add(nc.vector, 512, 512)
+        store(512, 512)
+        add(nc.vector, 1024, 256)
+        store(1024, 256)
+        fetch_and_weigh(1408, 128)
+        add(nc.vector, 1280, 128)
+        store(1280, 128)
+        add(nc.vector, 1408, 128)
+        store(1408, 128)

@@ -43,9 +43,9 @@ BATCHES = (
     ((11, 256, 3, 0),),
     ((11, 128, 0, 0),),
 )
-FUSED = 1280
+FUSED = 1152
 FUSED_AHEAD = 896
-SUMS_ON_GPSIMD = (256, 256)
+SUMS_ON_GPSIMD = (416,)
 
 
 def widths(slots):
@@ -132,9 +132,11 @@ def tile_moe_rag_lin_relu_kernel(tc, xT, w_words, w_scales, b, gate, offs, pos1,
 
         banks = [psum.tile([P, BANK], F32, name=f"bank{i}") for i in range(8)]
         order = [(1, t) for t in range(0, FUSED, P)] + [(c, t) for t in range(FUSED, T, P) for c in range(2)]
+        order.insert(11, None)
         nc.tensor.transpose(banks[0][:, :P], gate_rows[:], identity[:])
         nc.scalar.copy(gate_cols[:], banks[0][:, :blocks])
-        for i, (c, t) in enumerate(order):
+        for i in [i for i in range(len(order)) if order[i]]:
+            c, t = order[i]
             r = (t - FUSED + c * T) // P
             nc.tensor.transpose(banks[4 + i // 4][:, i % 4 * P : (i % 4 + 1) * P], gate_cols[:, r : r + 1].to_broadcast([P, P]), identity[:])
         for s0 in (0, S // 2):
@@ -195,10 +197,11 @@ def tile_moe_rag_lin_relu_kernel(tc, xT, w_words, w_scales, b, gate, offs, pos1,
             store(t0, n)
             t0 += n
         fetch_and_weigh(512, 512)
-        fetch_and_weigh(1024, 256)
+        fetch_and_weigh(1024, 128)
+        fetch_and_weigh(1152, 128)
+        add(nc.vector, t0, 1024 - t0)
+        store(t0, 1024 - t0)
         fetch_and_weigh(1280, 128)
-        add(nc.vector, 512, 512)
-        store(512, 512)
         add(nc.vector, 1024, 256)
         store(1024, 256)
         fetch_and_weigh(1408, 128)

@@ -43,9 +43,14 @@ BATCHES = (
     ((11, 256, 3, 0),),
     ((11, 128, 0, 0),),
 )
-FUSED = 1152
-FUSED_AHEAD = 896
-SUMS_ON_GPSIMD = (416,)
+FUSED = (704, 576)
+SPREAD = (
+    tuple((1, t) for t in range(512, 1024, P)),
+    tuple((0, t) for t in range(640, 1024, P)),
+    ((0, 1024), (0, 1152), (1, 1024), (1, 1152)),
+    ((0, 1280), (0, 1408), (1, 1280), (1, 1408)),
+)
+PAIRED = ((1024, 256), (1280, 160), (1440, 96))
 
 
 def widths(slots):
@@ -70,10 +75,10 @@ def tile_moe_rag_lin_relu_kernel(tc, xT, w_words, w_scales, b, gate, offs, pos1,
         wt = keep.tile([P, E, 2 * N], U8, name="wt", align_bytes=64)
         wt_scales = keep.tile([P, E, N], U8, name="wt_scales", align_bytes=64)
         bias = keep.tile([P, E], F32, name="bias")
-        gate0 = keep.tile([P, FUSED], F32, name="gate0")
+        gates = [keep.tile([P, FUSED[c]], F32, name=f"gates{c}") for c in range(2)]
+        blocks = sorted(block for bank in SPREAD for block in bank)
         gate_rows = keep.tile([P, P], F32, name="gate_rows")
-        blocks = (2 * T - FUSED) // P
-        gate_cols = keep.tile([P, blocks], F32, name="gate_cols")
+        gate_cols = keep.tile([P, len(blocks)], F32, name="gate_cols")
         identity = keep.tile([P, P], F32, name="identity")
         y = keep.tile([P, S], F32, name="y")
         fetched = keep.tile([P, 2, T], F32, name="fetched")
@@ -96,8 +101,9 @@ def tile_moe_rag_lin_relu_kernel(tc, xT, w_words, w_scales, b, gate, offs, pos1,
             nc.sync.dma_start(out=r[:], in_=rows[:, :, t0 : t0 + n])
             raw.append(r)
         nc.sync.dma_start(idx[:], offs)
-        flat = gate.rearrange("c n t -> (c n t)")
-        nc.sync.dma_start(out=gate_rows[:blocks, :], in_=flat[(N - 1) * T + FUSED : (N + 1) * T].rearrange("(r t) -> r t", t=P))
+        for c in range(2):
+            mine = [r for r, block in enumerate(blocks) if block[0] == c]
+            nc.sync.dma_start(out=gate_rows[mine[0] : mine[-1] + 1, :], in_=gate[c, 0, blocks[mine[0]][1] :].rearrange("(r t) -> r t", t=P))
         w_scales_i = w_scales.bitcast(I32)
         for q in range(4):
             nc.sync.dma_start(
@@ -108,7 +114,8 @@ def tile_moe_rag_lin_relu_kernel(tc, xT, w_words, w_scales, b, gate, offs, pos1,
         nc.sync.dma_start(out=bias[:], in_=b)
         nc.sync.dma_start(p1[:], pos1)
         nc.sync.dma_start(p2[:], pos2)
-        nc.sync.dma_start(out=gate0[:], in_=gate[0, :, :FUSED])
+        for c in range(2):
+            nc.sync.dma_start(out=gates[c][:], in_=gate[c, :, : FUSED[c]])
 
         grouped = keep.tile([P, T, PACK], BF16, name="grouped", align_bytes=64)
         for step, t0, n in HEAD:
@@ -131,14 +138,12 @@ def tile_moe_rag_lin_relu_kernel(tc, xT, w_words, w_scales, b, gate, offs, pos1,
             nc.vector.tensor_copy(dst[:, s0 : s0 + n], src[:].indirect(idx[:, s0 // PER_COLUMN : (s0 + n) // PER_COLUMN]))
 
         banks = [psum.tile([P, BANK], F32, name=f"bank{i}") for i in range(8)]
-        order = [(1, t) for t in range(0, FUSED, P)] + [(c, t) for t in range(FUSED, T, P) for c in range(2)]
-        order.insert(11, None)
         nc.tensor.transpose(banks[0][:, :P], gate_rows[:], identity[:])
-        nc.scalar.copy(gate_cols[:], banks[0][:, :blocks])
-        for i in [i for i in range(len(order)) if order[i]]:
-            c, t = order[i]
-            r = (t - FUSED + c * T) // P
-            nc.tensor.transpose(banks[4 + i // 4][:, i % 4 * P : (i % 4 + 1) * P], gate_cols[:, r : r + 1].to_broadcast([P, P]), identity[:])
+        nc.scalar.copy(gate_cols[:], banks[0][:, : len(blocks)])
+        for i, bank in enumerate(SPREAD):
+            for j, block in enumerate(bank):
+                r = blocks.index(block)
+                nc.tensor.transpose(banks[4 + i][:, j * P : (j + 1) * P], gate_cols[:, r : r + 1].to_broadcast([P, P]), identity[:])
         for s0 in (0, S // 2):
             gather_slots(slot_scales, scales, s0, S // 2)
         s0 = 0
@@ -171,41 +176,32 @@ def tile_moe_rag_lin_relu_kernel(tc, xT, w_words, w_scales, b, gate, offs, pos1,
         def entries(choice, t0, n):
             return y[:].indirect(pos[choice][:, t0 // PER_COLUMN : (t0 + n) // PER_COLUMN])
 
-        def fetch_and_weigh(t0, n):
-            first = 1 if t0 < FUSED else 0
-            for c in range(first, 2):
+        def fused(choice, t0, t1):
+            nc.vector.tensor_tensor(gated[:, choice, t0:t1], entries(choice, t0, t1 - t0), gates[choice][:, t0:t1], MULT)
+
+        def fetch_and_weigh(choices, t0, n):
+            for c in choices:
                 nc.scalar.activation(fetched[:, c, t0 : t0 + n], entries(c, t0, n), COPY)
-            i = order.index((first, t0))
-            gates = banks[4 + i // 4][:, i % 4 * P : i % 4 * P + (2 - first) * n].rearrange("p (c t) -> p c t", t=n)
-            nc.vector.tensor_tensor(gated[:, first:, t0 : t0 + n], fetched[:, first:, t0 : t0 + n], gates, MULT)
+            i = [k for k, bank in enumerate(SPREAD) if (choices[0], t0 // P * P) in bank][0]
+            c0 = t0 - SPREAD[i][0][1]
+            spread = banks[4 + i][:, : len(SPREAD[i]) * P].rearrange("p (c t) -> p c t", c=len(choices))[:, :, c0 : c0 + n]
+            planes = slice(choices[0], choices[-1] + 1)
+            nc.vector.tensor_tensor(gated[:, planes, t0 : t0 + n], fetched[:, planes, t0 : t0 + n], spread, MULT)
 
-        def fused(t0, t1):
-            nc.vector.tensor_tensor(gated[:, 0, t0:t1], entries(0, t0, t1 - t0), gate0[:, t0:t1], MULT)
-
-        def add(engine, t0, n):
+        def add_and_store(engine, t0, n):
             engine.tensor_tensor(total[:, t0 : t0 + n], gated[:, 0, t0 : t0 + n], gated[:, 1, t0 : t0 + n], ADD)
-
-        def store(t0, n):
             nc.sync.dma_start(out=out[:, t0 : t0 + n], in_=total[:, t0 : t0 + n])
 
-        fused(0, FUSED_AHEAD)
-        fetch_and_weigh(0, 512)
-        fused(FUSED_AHEAD, FUSED)
-        t0 = 0
-        for n in SUMS_ON_GPSIMD:
-            add(nc.gpsimd, t0, n)
-            store(t0, n)
-            t0 += n
-        fetch_and_weigh(512, 512)
-        fetch_and_weigh(1024, 128)
-        fetch_and_weigh(1152, 128)
-        add(nc.vector, t0, 1024 - t0)
-        store(t0, 1024 - t0)
-        fetch_and_weigh(1280, 128)
-        add(nc.vector, 1024, 256)
-        store(1024, 256)
-        fetch_and_weigh(1408, 128)
-        add(nc.vector, 1280, 128)
-        store(1280, 128)
-        add(nc.vector, 1408, 128)
-        store(1408, 128)
+        both = FUSED[1]
+        fused(1, 0, both)
+        fused(0, 0, both)
+        fused(0, both, FUSED[0])
+        add_and_store(nc.gpsimd, 0, both)
+        for c in (1, 0):
+            fetch_and_weigh((c,), FUSED[c], PAIRED[0][0] - FUSED[c])
+        waiting = (both, PAIRED[0][0] - both)
+        for t0, n in PAIRED:
+            fetch_and_weigh((0, 1), t0, n)
+            add_and_store(nc.vector, *waiting)
+            waiting = (t0, n)
+        add_and_store(nc.vector, *waiting)

@@ -38,11 +38,12 @@ SCALE_COLUMNS = 2048
 BATCHES = (
     ((0, 128, 0, 0), (1, 128, 0, 128), (2, 128, 0, 256), (3, 128, 0, 384), (4, 384, 1, 0), (5, 128, 1, 384)),
     ((6, 256, 2, 0), (7, 512, 3, 0)),
-    ((8, 128, 0, 0), (9, 256, 0, 128)),
-    ((10, 256, 1, 0), (10, 256, 2, 0)),
-    ((11, 256, 3, 0),),
+    ((8, 128, 4, 0), (9, 256, 4, 128)),
+    ((10, 256, 5, 0), (10, 256, 6, 0)),
+    ((11, 256, 7, 0),),
     ((11, 128, 0, 0),),
 )
+GATE_BANKS = (5, 6, 7, 0)
 FUSED = (704, 576)
 SPREAD = (
     tuple((1, t) for t in range(512, 1024, P)),
@@ -140,10 +141,6 @@ def tile_moe_rag_lin_relu_kernel(tc, xT, w_words, w_scales, b, gate, offs, pos1,
         banks = [psum.tile([P, BANK], F32, name=f"bank{i}") for i in range(8)]
         nc.tensor.transpose(banks[0][:, :P], gate_rows[:], identity[:])
         nc.scalar.copy(gate_cols[:], banks[0][:, : len(blocks)])
-        for i, bank in enumerate(SPREAD):
-            for j, block in enumerate(bank):
-                r = blocks.index(block)
-                nc.tensor.transpose(banks[4 + i][:, j * P : (j + 1) * P], gate_cols[:, r : r + 1].to_broadcast([P, P]), identity[:])
         for s0 in (0, S // 2):
             gather_slots(slot_scales, scales, s0, S // 2)
         s0 = 0
@@ -171,6 +168,11 @@ def tile_moe_rag_lin_relu_kernel(tc, xT, w_words, w_scales, b, gate, offs, pos1,
                 else:
                     nc.scalar.activation(y[:, a : a + m], banks[bank][:, c : c + m], RELU, bias=bias[:, e : e + 1])
 
+        for i, bank in enumerate(SPREAD):
+            for j, block in enumerate(bank):
+                r = blocks.index(block)
+                nc.tensor.transpose(banks[GATE_BANKS[i]][:, j * P : (j + 1) * P], gate_cols[:, r : r + 1].to_broadcast([P, P]), identity[:])
+
         pos = (p1, p2)
 
         def entries(choice, t0, n):
@@ -184,7 +186,7 @@ def tile_moe_rag_lin_relu_kernel(tc, xT, w_words, w_scales, b, gate, offs, pos1,
                 nc.scalar.activation(fetched[:, c, t0 : t0 + n], entries(c, t0, n), COPY)
             i = [k for k, bank in enumerate(SPREAD) if (choices[0], t0 // P * P) in bank][0]
             c0 = t0 - SPREAD[i][0][1]
-            spread = banks[4 + i][:, : len(SPREAD[i]) * P].rearrange("p (c t) -> p c t", c=len(choices))[:, :, c0 : c0 + n]
+            spread = banks[GATE_BANKS[i]][:, : len(SPREAD[i]) * P].rearrange("p (c t) -> p c t", c=len(choices))[:, :, c0 : c0 + n]
             planes = slice(choices[0], choices[-1] + 1)
             nc.vector.tensor_tensor(gated[:, planes, t0 : t0 + n], fetched[:, planes, t0 : t0 + n], spread, MULT)
 

@@ -44,14 +44,14 @@ BATCHES = (
     ((11, 128, 0, 0),),
 )
 GATE_BANKS = (5, 6, 7, 0)
-FUSED = (704, 576)
+FUSED = (672, 576)
 SPREAD = (
     tuple((1, t) for t in range(512, 1024, P)),
     tuple((0, t) for t in range(640, 1024, P)),
     ((0, 1024), (0, 1152), (1, 1024), (1, 1152)),
     ((0, 1280), (0, 1408), (1, 1280), (1, 1408)),
 )
-PAIRED = ((1024, 256), (1280, 160), (1440, 96))
+PAIRED = ((1024, 256), (1280, 192), (1472, 64))
 
 
 def widths(slots):

from contextlib import ExitStack

import concourse.mybir as mybir
from concourse.masks import make_identity

K, T, E, N = 512, 1536, 12, 128
S = 2 * T

P = 128
PACK = 4
PER_COLUMN = 16
BANK = 512
F32 = mybir.dt.float32
BF16 = mybir.dt.bfloat16
U32 = mybir.dt.uint32
I32 = mybir.dt.int32
U16 = mybir.dt.uint16
U8 = mybir.dt.uint8
E4M3X4 = mybir.dt.float8_e4m3fn_x4
E2M1X4 = mybir.dt.float4_e2m1fn_x4
COPY = mybir.ActivationFunctionType.Copy
RELU = mybir.ActivationFunctionType.Relu
ADD = mybir.AluOpType.add
MAX = mybir.AluOpType.max
MULT = mybir.AluOpType.mult

FLOPS = 2 * S * K * N

LOADS = ((0, 896), (896, 512), (1408, 128))
HEAD = (
    ("scalar", 0, 192), ("vector", 192, 320), ("vector", 512, 192), ("scalar", 704, 192),
    ("quantise", 0, 512), ("quantise", 512, 256), ("quantise", 768, 128),
    ("vector", 896, 256), ("vector", 1152, 48), ("scalar", 1200, 208), ("quantise", 896, 256),
    ("vector", 1408, 64), ("scalar", 1472, 64), ("quantise", 1152, 256), ("quantise", 1408, 128),
)
NEIGHBOURS = 2
SCALE_COLUMNS = 2048
BATCHES = (
    ((0, 128, 0, 0), (1, 128, 0, 128), (2, 128, 0, 256), (3, 128, 0, 384), (4, 384, 1, 0), (5, 128, 1, 384)),
    ((6, 256, 2, 0), (7, 512, 3, 0)),
    ((8, 128, 4, 0), (9, 256, 4, 128)),
    ((10, 256, 5, 0), (10, 256, 6, 0)),
    ((11, 256, 7, 0),),
    ((11, 128, 0, 0),),
)
GATE_BANKS = (5, 6, 7, 0)
FUSED = (672, 576)
SPREAD = (
    tuple((1, t) for t in range(512, 1024, P)),
    tuple((0, t) for t in range(640, 1024, P)),
    ((0, 1024), (0, 1152), (1, 1024), (1, 1152)),
    ((0, 1280), (0, 1408), (1, 1280), (1, 1408)),
)
PAIRED = ((1024, 256), (1280, 192), (1472, 64))


def widths(slots):
    return (256, 128) if slots == 384 else (slots,)


def tile_moe_rag_lin_relu_kernel(tc, xT, w_words, w_scales, b, gate, offs, pos1, pos2, out):
    nc = tc.nc
    with ExitStack() as ctx:
        lists = ctx.enter_context(tc.tile_pool(name="lists", bufs=1))
        keep = ctx.enter_context(tc.tile_pool(name="keep", bufs=1))
        psum = ctx.enter_context(tc.psum_pool(name="psum", bufs=1))

        idx = lists.tile([P, S // PER_COLUMN], U16, name="idx")
        p1 = lists.tile([P, T // PER_COLUMN], U16, name="p1")
        p2 = lists.tile([P, T // PER_COLUMN], U16, name="p2")

        codes = keep.tile([P, T], U32, name="codes", align_bytes=64)
        scales = keep.tile([P, SCALE_COLUMNS], U8, name="scales", align_bytes=64)
        slot_codes = keep.tile([P, S], U32, name="slot_codes", align_bytes=64)
        slot_scales = keep.tile([P, S], U8, name="slot_scales", align_bytes=64)
        wt = keep.tile([P, E, 2 * N], U8, name="wt", align_bytes=64)
        wt_scales = keep.tile([P, E, N], U8, name="wt_scales", align_bytes=64)
        bias = keep.tile([P, E], F32, name="bias")
        gates = [keep.tile([P, FUSED[c]], F32, name=f"gates{c}") for c in range(2)]
        blocks = sorted(block for bank in SPREAD for block in bank)
        gate_rows = keep.tile([P, P], F32, name="gate_rows")
        gate_cols = keep.tile([P, len(blocks)], F32, name="gate_cols")
        identity = keep.tile([P, P], F32, name="identity")
        y = keep.tile([P, S], F32, name="y")
        fetched = keep.tile([P, 2, T], F32, name="fetched")
        gated = keep.tile([P, 2, T], F32, name="gated")
        total = keep.tile([P, T], F32, name="total")
        warm = keep.tile([P, 1], F32, name="warm")

        nc.gpsimd.memset(warm[:], 0.0)
        nc.scalar.activation(warm[:], warm[:], RELU)
        nc.gpsimd.memset(scales[:], 0)
        nc.vector.memset(wt_scales[:].rearrange("p e n -> p (e n)").bitcast(I32), 0)

        nc.gpsimd.memset(gate_rows[:], 0.0)
        make_identity(nc, identity[:])

        rows = xT.rearrange("(p j) t -> p j t", j=PACK)
        raw = []
        for i, (t0, n) in enumerate(LOADS):
            r = keep.tile([P, PACK, n], F32, name=f"raw{i}")
            nc.sync.dma_start(out=r[:], in_=rows[:, :, t0 : t0 + n])
            raw.append(r)
        nc.sync.dma_start(idx[:], offs)
        for c in range(2):
            mine = [r for r, block in enumerate(blocks) if block[0] == c]
            nc.sync.dma_start(out=gate_rows[mine[0] : mine[-1] + 1, :], in_=gate[c, 0, blocks[mine[0]][1] :].rearrange("(r t) -> r t", t=P))
        w_scales_i = w_scales.bitcast(I32)
        for q in range(4):
            nc.sync.dma_start(
                out=wt_scales[32 * q : 32 * q + 4].bitcast(I32),
                in_=w_scales_i[:, 0, 4 * q : 4 * q + 4, :].rearrange("e q n -> q e n"),
            )
        nc.sync.dma_start(out=wt[:].bitcast(I32), in_=w_words.bitcast(I32).rearrange("e a p c -> p (e a) c"))
        nc.sync.dma_start(out=bias[:], in_=b)
        nc.sync.dma_start(p1[:], pos1)
        nc.sync.dma_start(p2[:], pos2)
        for c in range(2):
            nc.sync.dma_start(out=gates[c][:], in_=gate[c, :, : FUSED[c]])

        grouped = keep.tile([P, T, PACK], BF16, name="grouped", align_bytes=64)
        for step, t0, n in HEAD:
            if step == "quantise":
                nc.vector.quantize_mx(
                    out=codes[:, t0 : t0 + n].bitcast(E4M3X4),
                    scales=scales[:, t0 : t0 + n],
                    in_=grouped[:, t0 : t0 + n, :].rearrange("p t j -> p (t j)"),
                )
            else:
                load = max(i for i, (first, count) in enumerate(LOADS) if first <= t0)
                c = t0 - LOADS[load][0]
                copy = nc.vector.tensor_copy if step == "vector" else nc.scalar.copy
                copy(
                    grouped[:, t0 : t0 + n, :].rearrange("p (q i) j -> p q j i", i=NEIGHBOURS),
                    raw[load][:, :, c : c + n].rearrange("p j (q i) -> p q j i", i=NEIGHBOURS),
                )

        def gather_slots(dst, src, s0, n):
            nc.vector.tensor_copy(dst[:, s0 : s0 + n], src[:].indirect(idx[:, s0 // PER_COLUMN : (s0 + n) // PER_COLUMN]))

        banks = [psum.tile([P, BANK], F32, name=f"bank{i}") for i in range(8)]
        nc.tensor.transpose(banks[0][:, :P], gate_rows[:], identity[:])
        nc.scalar.copy(gate_cols[:], banks[0][:, : len(blocks)])
        for s0 in (0, S // 2):
            gather_slots(slot_scales, scales, s0, S // 2)
        s0 = 0
        for batch in BATCHES:
            gather_slots(slot_codes, codes, s0, sum(run[1] for run in batch))
            starts = []
            for e, m, bank, c in batch:
                starts.append(s0)
                d = 0
                for w in widths(m):
                    nc.tensor.matmul_mx(
                        out=banks[bank][:, c + d : c + d + w],
                        lhsT=wt[:, e, :].bitcast(E2M1X4),
                        lhsT_scale=wt_scales[:, e, :],
                        rhs=slot_codes[:, s0 + d : s0 + d + w].bitcast(E4M3X4),
                        rhs_scale=slot_scales[:, s0 + d : s0 + d + w],
                        start=True,
                        stop=True,
                    )
                    d += w
                s0 += m
            for a, (e, m, bank, c) in zip(starts, batch):
                if batch == BATCHES[-2]:
                    nc.vector.tensor_scalar(y[:, a : a + m], banks[bank][:, c : c + m], bias[:, e : e + 1], 0.0, ADD, MAX)
                else:
                    nc.scalar.activation(y[:, a : a + m], banks[bank][:, c : c + m], RELU, bias=bias[:, e : e + 1])

        for i, bank in enumerate(SPREAD):
            for j, block in enumerate(bank):
                r = blocks.index(block)
                nc.tensor.transpose(banks[GATE_BANKS[i]][:, j * P : (j + 1) * P], gate_cols[:, r : r + 1].to_broadcast([P, P]), identity[:])

        pos = (p1, p2)

        def entries(choice, t0, n):
            return y[:].indirect(pos[choice][:, t0 // PER_COLUMN : (t0 + n) // PER_COLUMN])

        def fused(choice, t0, t1):
            nc.vector.tensor_tensor(gated[:, choice, t0:t1], entries(choice, t0, t1 - t0), gates[choice][:, t0:t1], MULT)

        def fetch_and_weigh(choices, t0, n):
            for c in choices:
                nc.scalar.activation(fetched[:, c, t0 : t0 + n], entries(c, t0, n), COPY)
            i = [k for k, bank in enumerate(SPREAD) if (choices[0], t0 // P * P) in bank][0]
            c0 = t0 - SPREAD[i][0][1]
            spread = banks[GATE_BANKS[i]][:, : len(SPREAD[i]) * P].rearrange("p (c t) -> p c t", c=len(choices))[:, :, c0 : c0 + n]
            planes = slice(choices[0], choices[-1] + 1)
            nc.vector.tensor_tensor(gated[:, planes, t0 : t0 + n], fetched[:, planes, t0 : t0 + n], spread, MULT)

        def add_and_store(engine, t0, n):
            engine.tensor_tensor(total[:, t0 : t0 + n], gated[:, 0, t0 : t0 + n], gated[:, 1, t0 : t0 + n], ADD)
            nc.sync.dma_start(out=out[:, t0 : t0 + n], in_=total[:, t0 : t0 + n])

        both = FUSED[1]
        fused(1, 0, both)
        fused(0, 0, both)
        fused(0, both, FUSED[0])
        add_and_store(nc.gpsimd, 0, both)
        for c in (1, 0):
            fetch_and_weigh((c,), FUSED[c], PAIRED[0][0] - FUSED[c])
        waiting = (both, PAIRED[0][0] - both)
        for t0, n in PAIRED:
            fetch_and_weigh((0, 1), t0, n)
            add_and_store(nc.vector, *waiting)
            waiting = (t0, n)
        add_and_store(nc.vector, *waiting)
